import numpy as np
import ml_dtypes


def mxq(x, axis, fmt="e4m3"):
    dtype, down = {"e4m3": (ml_dtypes.float8_e4m3fn, 7), "e5m2": (ml_dtypes.float8_e5m2, 14)}[fmt]
    v = np.moveaxis(np.asarray(x, np.float32).astype(ml_dtypes.bfloat16).astype(np.float64), axis, -1)
    blocks = v.reshape(v.shape[:-1] + (-1, 32))
    amax = np.abs(blocks).max(-1, keepdims=True)
    byte = np.maximum(np.where(amax > 0, np.frexp(amax)[1] - 1 + 127, 0) - down, 1)
    scale = np.exp2(byte - 127.0)
    codes = (blocks / scale).astype(np.float32).astype(dtype).astype(np.float64)
    return np.moveaxis((codes * scale).reshape(v.shape), -1, axis)


WIDE = False


def mx_kscale(k):
    if not WIDE:
        return np.ones(k)
    levels = np.array([10, -10, 5, -5, 0])
    if k % 512:
        return np.exp2(np.random.permutation(np.resize(levels, k // 32))).repeat(32)
    a = np.empty((k // 512, 16))
    for p in range(k // 512):
        a[p, :8] = np.random.permutation(np.resize(levels, 8))
        for g in range(8):
            far = levels[np.abs(levels - a[p, g]) >= 10]
            a[p, g + 8] = far[np.random.randint(len(far))]
    return np.exp2(a.ravel()).repeat(32)


def f64(x):
    return np.asarray(x).astype(np.float64)


def striped(idx):
    return np.tile(idx.reshape(-1, 16).T, (8, 1)).astype(np.uint16)


def unstriped(offs):
    return offs[:16].T.reshape(-1).astype(np.int64)


def striped8(idx):
    return np.concatenate([x.reshape(-1, 16).T for x in idx]).astype(np.uint16)


def runs(offs, k):
    lists = np.stack([offs[16 * r : 16 * r + 16].T.reshape(-1) for r in range(8)]).astype(np.int64)
    return lists[np.arange(k) % 512 // 64]


def pack_weight(w):
    k, n = w.shape
    w = f64(np.asarray(w, np.float32).astype(ml_dtypes.bfloat16)).reshape(k // 32, 32, n)
    amax = np.abs(w).max(1)
    byte = np.clip(np.where(amax > 0, np.frexp(amax)[1] - 1 + 127 - 7, 1), 1, 254)
    scaled = (w * np.exp2(127.0 - byte)[:, None, :]).reshape(k, n).astype(np.float32)
    words = np.ascontiguousarray(scaled.reshape(k // 512, 128, 4, n).transpose(0, 1, 3, 2)).astype(ml_dtypes.float8_e4m3fn).view(np.uint8)
    return words, np.ascontiguousarray(byte.astype(np.uint8).reshape(k // 512, 16, n))


def unpack_weight(words, scales):
    g, p, n, _ = words.shape
    vals = np.ascontiguousarray(words).view(ml_dtypes.float8_e4m3fn).astype(np.float64) * np.repeat(np.exp2(scales.astype(np.float64) - 127.0), 8, axis=1)[..., None]
    return vals.transpose(0, 1, 3, 2).reshape(g * 512, n)

def planes(y):
    n, m = y.shape
    v = y.astype(np.float32).astype(ml_dtypes.bfloat16).astype(np.float64).reshape(n // 32, 32, m)
    top = np.abs(v).max(1)
    byte = np.clip(np.where(top > 0, np.frexp(top)[1] - 1 + 127 - 7, 1), 1, 254)
    codes = (v * np.exp2(127.0 - byte)[:, None, :]).reshape(n, m).astype(np.float32).astype(ml_dtypes.float8_e4m3fn).view(np.uint8)
    words = codes.reshape(n // 512, 128, 4, m).transpose(0, 1, 3, 2)
    return np.ascontiguousarray(words), np.ascontiguousarray(byte.astype(np.uint8).reshape(n // 512, 16, m))


K, T, S, N, G, H, U = 512, 2048, 512, 512, 2048, 512, 512


def setup_inputs():
    n = np.random.standard_normal
    s = mx_kscale(K)[:, None]
    u = mx_kscale(H)
    packed_xT = pack_weight(n((K, T)) * s)
    packed_dT = pack_weight(n((K, G)) / s)
    packed_w1 = pack_weight(n((H, N)) / np.sqrt(H) / u[:, None])
    return {
        "x_words": packed_xT[0],
        "x_scales": packed_xT[1],
        "d_words": packed_dT[0],
        "d_scales": packed_dT[1],
        "temp": np.random.uniform(0.3, 1.5, (H, U)).astype(np.float32),
        "gn": (np.random.uniform(0.5, 1.5, (H, 1)) * u[:, None]).astype(np.float32),
        "w1_words": packed_w1[0],
        "w1_scales": packed_w1[1],
        "offs": striped(np.random.permutation(T)[:S]),
        "kidx": striped8(np.random.randint(0, G, (8, H))),
        "task": striped8(np.stack([np.random.permutation(U)[(U * np.random.uniform(0, 1, S) ** 4).astype(np.int64)] for _ in range(8)])),
    }


def reference(x_words, x_scales, d_words, d_scales, temp, gn, w1_words, w1_scales, offs, kidx, task):
    d_kidx = unpack_weight(d_words, d_scales)[np.arange(K)[:, None], runs(kidx, K)]
    xq = unpack_weight(x_words, x_scales)[:, unstriped(offs)]
    s = 0.0625 * (d_kidx.T @ xq)
    z = f64(gn) * (np.tanh(s * (f64(temp)[np.arange(H)[:, None], runs(task, H)])))
    out_0 = unpack_weight(w1_words, w1_scales).T @ mxq(z, 0, "e4m3")
    return (out_0,) + planes(out_0)

@@ -1,0 +1,209 @@
+from contextlib import ExitStack
+
+import concourse.mybir as mybir
+
+F32 = mybir.dt.float32
+BF16 = mybir.dt.bfloat16
+I32 = mybir.dt.int32
+U32 = mybir.dt.uint32
+U16 = mybir.dt.uint16
+U8 = mybir.dt.uint8
+FP8X4 = mybir.dt.float8_e4m3fn_x4
+ACT = mybir.ActivationFunctionType
+MULT = mybir.AluOpType.mult
+
+P = 128
+PACK = 4
+TABLE = 2048
+S = 512
+CH = 128
+GW = 256
+FLOPS = 2 * 2 * 512 * 512 * 512
+
+
+def words_of(dram):
+    return dram[0].rearrange("p n t -> p (n t)").bitcast(I32)
+
+
+def tile_picked_temper_tanh_po_kernel(
+    tc, x_words, x_scales, d_words, d_scales, temp, gn, w1_words, w1_scales, offs, kidx, task, out_0, out_1, out_2
+):
+    nc = tc.nc
+    with ExitStack() as ctx:
+        keep = ctx.enter_context(tc.tile_pool(name="keep", bufs=1))
+        reuse = ctx.enter_context(tc.tile_pool(name="reuse", bufs=1))
+        psum = ctx.enter_context(tc.psum_pool(name="psum", bufs=1))
+
+        def sb(name, shape, dtype):
+            return keep.tile(shape, dtype, name=name, align_bytes=64)
+
+        kidx_sb = sb("kidx_sb", [P, S // 16], U16)
+        offs_sb = sb("offs_sb", [P, S // 16], U16)
+        task_sb = sb("task_sb", [P, S // 16], U16)
+        dsc_win = sb("dsc_win", [P, TABLE], U8)
+        xsc_win = reuse.tile([P, TABLE], U8, name="xsc_win", offset=0)
+        warm = sb("warm", [P, 1], F32)
+        dw_win = reuse.tile([P, TABLE], I32, name="dw_win", offset=TABLE)
+        xw_win = sb("xw_win", [P, TABLE], I32)
+        placed = sb("placed", [P, 2 * S], U8)
+        warm_out = sb("warm_out", [P, 1], F32)
+
+        nc.vector.memset(placed[:].bitcast(I32), 0)
+
+        def spread(scales):
+            return scales[0].bitcast(I32).unsqueeze(1).to_broadcast([16, 8, TABLE // 4])
+
+        gn_sb = sb("gn_sb", [P, PACK], F32)
+        nc.sync.dma_start(kidx_sb[:], kidx)
+        nc.scalar.dma_start(dsc_win[:].bitcast(I32), spread(d_scales))
+        nc.sync.dma_start(offs_sb[:], offs)
+        nc.scalar.dma_start(xsc_win[:].bitcast(I32), spread(x_scales))
+        nc.sync.dma_start(task_sb[:], task)
+        nc.scalar.dma_start(gn_sb[:], gn.rearrange("(p t) o -> p (t o)", t=PACK))
+        nc.sync.dma_start(dw_win[:], words_of(d_words))
+        nc.sync.dma_start(xw_win[:], words_of(x_words))
+        ww_raw = sb("ww_raw", [P, S], I32)
+        nc.sync.dma_start(ww_raw[:], words_of(w1_words))
+        nc.vector.memset(warm[:], 0.0)
+        nc.scalar.activation(warm_out[:], warm[:], ACT.Tanh)
+        temp_rows = temp.rearrange("(p t) u -> p t u", t=PACK)
+        temp_sb = []
+
+        def deal(dst, src):
+            nc.vector.tensor_copy(dst.rearrange("p (t m) -> p t m", t=PACK), src.rearrange("p (m t) -> p t m", t=PACK))
+
+        picked = sb("picked", [P, 2 * S], U8)
+        nc.vector.tensor_copy(picked[:, :S], dsc_win[:].indirect(kidx_sb[:]))
+        nc.vector.tensor_copy(picked[:, S:], xsc_win[:].indirect(offs_sb[:]))
+        for q in range(4):
+            nc.scalar.dma_start(placed[32 * q : 32 * q + 4, :].bitcast(I32), picked[32 * q : 32 * q + 32 : 8, :].bitcast(I32))
+        xsc = placed[:, S:]
+        dw_g = sb("dw_g", [P, S], U32)
+        nc.vector.tensor_copy(dw_g[:], dw_win[:].bitcast(U32).indirect(kidx_sb[:]))
+        dw = sb("dw", [P, S], U32)
+        deal(dw[:].bitcast(I32), dw_g[:].bitcast(I32))
+        for t in range(PACK):
+            tt = reuse.tile([P, S], F32, name=f"temp{t}", offset=t * TABLE)
+            nc.sync.dma_start(tt[:], temp_rows[:, t, :])
+            temp_sb.append(tt)
+        wsc_raw = reuse.tile([P, S], U8, name="wsc_raw", offset=PACK * TABLE)
+        for q in range(4):
+            nc.sync.dma_start(
+                wsc_raw[32 * q : 32 * q + 32, :].bitcast(I32),
+                w1_scales[0, 4 * q : 4 * q + 4, :].bitcast(I32).unsqueeze(0).to_broadcast([8, 4, S // 4]),
+            )
+        xw = [sb(f"xw{h}", [P, GW], U32) for h in range(S // GW)]
+
+        def queries(h):
+            nc.vector.tensor_copy(xw[h][:], xw_win[:].bitcast(U32).indirect(offs_sb[:, h * GW // 16 : (h + 1) * GW // 16]))
+
+        dsc = sb("dsc", [P, S], U8)
+
+        ww = sb("ww", [P, S], U32)
+        wsc = sb("wsc", [P, S], U8)
+        y_scales = sb("y_scales", [P, S], U8)
+        out_rows = out_0.rearrange("(p t) j -> p t j", t=PACK)
+        out_words = words_of(out_1)
+        per = GW // CH
+        spans = [(0, 128), (128, 256), (384, 128)]
+        s_sb = [sb(f"s{g}", [P, PACK, w], F32) for g, (lo, w) in enumerate(spans)]
+        u_sb = [sb(f"u{g}", [P, PACK, w], F32) for g, (lo, w) in enumerate(spans)]
+
+        def span_of(c):
+            g = max(g for g, (lo, w) in enumerate(spans) if lo <= c * CH)
+            return g, c * CH - spans[g][0]
+
+        zq = {}
+
+        def scores(c):
+            h, lo = c // per, (c % per) * CH
+            bank = psum.tile([P, PACK, CH], F32, name=f"s_bank{c}")
+            for t in range(PACK):
+                nc.tensor.matmul_mx(
+                    out=bank[:, t, :],
+                    lhsT=dw[:, t * P : (t + 1) * P].bitcast(FP8X4),
+                    lhsT_scale=dsc[:, t * P : (t + 1) * P],
+                    rhs=xw[h][:, lo : lo + CH].bitcast(FP8X4),
+                    rhs_scale=xsc[:, c * CH : (c + 1) * CH],
+                    start=True,
+                    stop=True,
+                )
+            g, at = span_of(c)
+            nc.scalar.copy(s_sb[g][:, :, at : at + CH], bank[:])
+
+        def temper(g):
+            lo, w = spans[g]
+            for t in range(PACK):
+                nc.vector.tensor_tensor(
+                    u_sb[g][:, t, :], temp_sb[t][:].indirect(task_sb[:, lo // 16 : (lo + w) // 16]), s_sb[g][:, t, :], MULT
+                )
+
+        def hidden(c):
+            g, at = span_of(c)
+            th = sb(f"th{c}", [P, CH, PACK], F32)
+            nc.scalar.activation(
+                th[:].rearrange("p (c i) t -> p c t i", i=4),
+                u_sb[g][:, :, at : at + CH].rearrange("p t (c i) -> p c t i", i=4),
+                ACT.Tanh,
+                scale=0.0625,
+            )
+            zb = sb(f"zb{c}", [P, CH, PACK], BF16)
+            nc.vector.tensor_tensor(zb[:], th[:], gn_sb[:].unsqueeze(1).to_broadcast([P, CH, PACK]), MULT)
+            zq[c] = zb
+
+        def values(c):
+            zw = sb(f"zw{c}", [P, CH], U32)
+            zs = sb(f"zs{c}", [P, CH], U8)
+            nc.vector.quantize_mx(out=zw[:].bitcast(FP8X4), scales=zs[:], in_=zq[c][:].rearrange("p j t -> p (j t)"))
+            bank = psum.tile([P, PACK, CH], F32, name=f"y_bank{c}")
+            for t in range(PACK):
+                nc.tensor.matmul_mx(
+                    out=bank[:, t, :],
+                    lhsT=ww[:, t * P : (t + 1) * P].bitcast(FP8X4),
+                    lhsT_scale=wsc[:, t * P : (t + 1) * P],
+                    rhs=zw[:].bitcast(FP8X4),
+                    rhs_scale=zs[:],
+                    start=True,
+                    stop=True,
+                )
+            yb = sb(f"yb{c}", [P, CH, PACK], BF16)
+            nc.scalar.copy(yb[:], bank[:].rearrange("p t j -> p j t"))
+            y = sb(f"y{c}", [P, PACK, CH], F32)
+            nc.scalar.copy(y[:], bank[:])
+            nc.sync.dma_start(out_rows[:, :, c * CH : (c + 1) * CH], y[:])
+            zq[c] = yb
+
+        def planes(c):
+            yw = sb(f"yw{c}", [P, CH], I32)
+            nc.vector.quantize_mx(
+                out=yw[:].bitcast(FP8X4), scales=y_scales[:, c * CH : (c + 1) * CH], in_=zq[c][:].rearrange("p j t -> p (j t)")
+            )
+            nc.sync.dma_start(out_words[:, c * CH : (c + 1) * CH], yw[:])
+
+        deal(dsc[:], placed[:, :S])
+        queries(0)
+        scores(0)
+        scores(1)
+        queries(1)
+        scores(2)
+        scores(3)
+        deal(ww[:].bitcast(I32), ww_raw[:])
+        temper(0)
+        hidden(0)
+        deal(wsc[:], wsc_raw[:])
+        values(0)
+        temper(1)
+        hidden(1)
+        planes(0)
+        values(1)
+        hidden(2)
+        values(2)
+        temper(2)
+        planes(1)
+        hidden(3)
+        values(3)
+        planes(2)
+        planes(3)
+        for q in range(4):
+            eng = nc.sync if q % 2 else nc.scalar
+            eng.dma_start(out_2[0, 4 * q : 4 * q + 4, :].bitcast(I32), y_scales[32 * q : 32 * q + 4, :].bitcast(I32))

@@ -31,6 +31,7 @@ def tile_picked_temper_tanh_po_kernel(
     nc = tc.nc
     with ExitStack() as ctx:
         keep = ctx.enter_context(tc.tile_pool(name="keep", bufs=1))
+        ring = ctx.enter_context(tc.tile_pool(name="ring", bufs=1))
         reuse = ctx.enter_context(tc.tile_pool(name="reuse", bufs=1))
         psum = ctx.enter_context(tc.psum_pool(name="psum", bufs=1))
 
@@ -41,79 +42,71 @@ def tile_picked_temper_tanh_po_kernel(
         offs_sb = sb("offs_sb", [P, S // 16], U16)
         task_sb = sb("task_sb", [P, S // 16], U16)
         dsc_win = sb("dsc_win", [P, TABLE], U8)
-        xsc_win = reuse.tile([P, TABLE], U8, name="xsc_win", offset=0)
+        xsc_win = sb("xsc_win", [P, TABLE], U8)
+        wsc_raw = sb("wsc_raw", [P, S], U8)
         warm = sb("warm", [P, 1], F32)
-        dw_win = reuse.tile([P, TABLE], I32, name="dw_win", offset=TABLE)
+        dw_win = reuse.tile([P, TABLE], I32, name="dw_win", offset=3 * TABLE)
         xw_win = sb("xw_win", [P, TABLE], I32)
-        placed = sb("placed", [P, 2 * S], U8)
         warm_out = sb("warm_out", [P, 1], F32)
 
-        nc.vector.memset(placed[:].bitcast(I32), 0)
 
         def spread(scales):
-            return scales[0].bitcast(I32).unsqueeze(1).to_broadcast([16, 8, TABLE // 4])
+            rows = scales[0].bitcast(I32)
+            return rows.unsqueeze(1).to_broadcast([16, 8, rows.shape[1]])
 
-        gn_sb = sb("gn_sb", [P, PACK], F32)
         nc.sync.dma_start(kidx_sb[:], kidx)
         nc.scalar.dma_start(dsc_win[:].bitcast(I32), spread(d_scales))
         nc.sync.dma_start(offs_sb[:], offs)
         nc.scalar.dma_start(xsc_win[:].bitcast(I32), spread(x_scales))
         nc.sync.dma_start(task_sb[:], task)
-        nc.scalar.dma_start(gn_sb[:], gn.rearrange("(p t) o -> p (t o)", t=PACK))
+        nc.scalar.dma_start(wsc_raw[:].bitcast(I32), spread(w1_scales))
         nc.sync.dma_start(dw_win[:], words_of(d_words))
         nc.sync.dma_start(xw_win[:], words_of(x_words))
-        ww_raw = sb("ww_raw", [P, S], I32)
-        nc.sync.dma_start(ww_raw[:], words_of(w1_words))
         nc.vector.memset(warm[:], 0.0)
         nc.scalar.activation(warm_out[:], warm[:], ACT.Tanh)
-        temp_rows = temp.rearrange("(p t) u -> p t u", t=PACK)
-        temp_sb = []
 
         def deal(dst, src):
-            nc.vector.tensor_copy(dst.rearrange("p (t m) -> p t m", t=PACK), src.rearrange("p (m t) -> p t m", t=PACK))
+            nc.vector.tensor_copy(dst.rearrange("p (t m) -> p m t", t=PACK), src.rearrange("p (m t) -> p m t", t=PACK))
 
-        picked = sb("picked", [P, 2 * S], U8)
-        nc.vector.tensor_copy(picked[:, :S], dsc_win[:].indirect(kidx_sb[:]))
-        nc.vector.tensor_copy(picked[:, S:], xsc_win[:].indirect(offs_sb[:]))
-        for q in range(4):
-            nc.scalar.dma_start(placed[32 * q : 32 * q + 4, :].bitcast(I32), picked[32 * q : 32 * q + 32 : 8, :].bitcast(I32))
-        xsc = placed[:, S:]
+        dsc_g = sb("dsc_g", [P, S], U8)
+        nc.vector.tensor_copy(dsc_g[:], dsc_win[:].indirect(kidx_sb[:]))
+        xsc_g = reuse.tile([P, S], U8, name="xsc_g", offset=2 * TABLE - S // 2)
+        nc.vector.tensor_copy(xsc_g[:], xsc_win[:].indirect(offs_sb[:]))
+        planes3 = sb("planes3", [P, 3 * S], U8)
+        dsc, wsc, xsc = planes3[:, :S], planes3[:, S : 2 * S], planes3[:, 2 * S :]
+        deal(dsc, dsc_g[:])
+        deal(wsc, wsc_raw[:])
+        nc.vector.tensor_copy(xsc.bitcast(I32), xsc_g[:].bitcast(I32))
+        for r in range(1, 4):
+            nc.sync.dma_start(planes3[r:P:32, :].bitcast(I32), planes3[8 * r : P : 32, :].bitcast(I32))
         dw_g = sb("dw_g", [P, S], U32)
         nc.vector.tensor_copy(dw_g[:], dw_win[:].bitcast(U32).indirect(kidx_sb[:]))
         dw = sb("dw", [P, S], U32)
         deal(dw[:].bitcast(I32), dw_g[:].bitcast(I32))
+        temp_rows = temp.rearrange("(p t) u -> p t u", t=PACK)
+        temp_sb = []
         for t in range(PACK):
-            tt = reuse.tile([P, S], F32, name=f"temp{t}", offset=t * TABLE)
+            tt = reuse.tile([P, S], F32, name=f"temp{t}", offset=(t + 1) * TABLE)
             nc.sync.dma_start(tt[:], temp_rows[:, t, :])
             temp_sb.append(tt)
-        wsc_raw = reuse.tile([P, S], U8, name="wsc_raw", offset=PACK * TABLE)
-        for q in range(4):
-            nc.sync.dma_start(
-                wsc_raw[32 * q : 32 * q + 32, :].bitcast(I32),
-                w1_scales[0, 4 * q : 4 * q + 4, :].bitcast(I32).unsqueeze(0).to_broadcast([8, 4, S // 4]),
-            )
+        ww_raw = reuse.tile([P, S], I32, name="ww_raw", offset=5 * TABLE)
+        nc.sync.dma_start(ww_raw[:], words_of(w1_words))
+        gn_sb = reuse.tile([P, PACK], F32, name="gn_sb", offset=6 * TABLE)
+        nc.sync.dma_start(gn_sb[:], gn.rearrange("(p t) o -> p (t o)", t=PACK))
         xw = [sb(f"xw{h}", [P, GW], U32) for h in range(S // GW)]
 
         def queries(h):
             nc.vector.tensor_copy(xw[h][:], xw_win[:].bitcast(U32).indirect(offs_sb[:, h * GW // 16 : (h + 1) * GW // 16]))
 
-        dsc = sb("dsc", [P, S], U8)
-
         ww = sb("ww", [P, S], U32)
-        wsc = sb("wsc", [P, S], U8)
         y_scales = sb("y_scales", [P, S], U8)
         out_rows = out_0.rearrange("(p t) j -> p t j", t=PACK)
         out_words = words_of(out_1)
         per = GW // CH
-        spans = [(0, 128), (128, 256), (384, 128)]
-        s_sb = [sb(f"s{g}", [P, PACK, w], F32) for g, (lo, w) in enumerate(spans)]
-        u_sb = [sb(f"u{g}", [P, PACK, w], F32) for g, (lo, w) in enumerate(spans)]
-
-        def span_of(c):
-            g = max(g for g, (lo, w) in enumerate(spans) if lo <= c * CH)
-            return g, c * CH - spans[g][0]
-
+        s_sb = {}
+        u_sb = {}
         zq = {}
+        y_bank = {}
 
         def scores(c):
             h, lo = c // per, (c % per) * CH
@@ -128,26 +121,34 @@ def tile_picked_temper_tanh_po_kernel(
                     start=True,
                     stop=True,
                 )
-            g, at = span_of(c)
-            nc.scalar.copy(s_sb[g][:, :, at : at + CH], bank[:])
+            if c == 0:
+                s_sb[c] = bank
+                return
+            s_sb[c] = sb(f"s{c}", [P, PACK, CH], F32)
+            nc.scalar.copy(s_sb[c][:], bank[:])
 
-        def temper(g):
-            lo, w = spans[g]
+        def temper(c):
+            u_sb[c] = ring.tile([P, PACK, CH], F32, name=f"u{c}", tag=f"slot{c}", align_bytes=64)
+            if c == 0:
+                tg = ring.tile([P, PACK, CH], F32, name="tg", tag="slot1", align_bytes=64)
+                for t in range(PACK):
+                    nc.vector.tensor_copy(tg[:, t, :], temp_sb[t][:].indirect(task_sb[:, : CH // 16]))
+                nc.vector.tensor_tensor(u_sb[c][:], s_sb[c][:], tg[:], MULT)
+                return
             for t in range(PACK):
                 nc.vector.tensor_tensor(
-                    u_sb[g][:, t, :], temp_sb[t][:].indirect(task_sb[:, lo // 16 : (lo + w) // 16]), s_sb[g][:, t, :], MULT
+                    u_sb[c][:, t, :], temp_sb[t][:].indirect(task_sb[:, c * CH // 16 : (c + 1) * CH // 16]), s_sb[c][:, t, :], MULT
                 )
 
         def hidden(c):
-            g, at = span_of(c)
             th = sb(f"th{c}", [P, CH, PACK], F32)
             nc.scalar.activation(
                 th[:].rearrange("p (c i) t -> p c t i", i=4),
-                u_sb[g][:, :, at : at + CH].rearrange("p t (c i) -> p c t i", i=4),
+                u_sb[c][:].rearrange("p t (c i) -> p c t i", i=4),
                 ACT.Tanh,
                 scale=0.0625,
             )
-            zb = sb(f"zb{c}", [P, CH, PACK], BF16)
+            zb = ring.tile([P, CH, PACK], BF16, name=f"zb{c}", tag=f"slot{c + 2}", align_bytes=64)
             nc.vector.tensor_tensor(zb[:], th[:], gn_sb[:].unsqueeze(1).to_broadcast([P, CH, PACK]), MULT)
             zq[c] = zb
 
@@ -168,10 +169,16 @@ def tile_picked_temper_tanh_po_kernel(
                 )
             yb = sb(f"yb{c}", [P, CH, PACK], BF16)
             nc.scalar.copy(yb[:], bank[:].rearrange("p t j -> p j t"))
-            y = sb(f"y{c}", [P, PACK, CH], F32)
-            nc.scalar.copy(y[:], bank[:])
-            nc.sync.dma_start(out_rows[:, :, c * CH : (c + 1) * CH], y[:])
             zq[c] = yb
+            y_bank[c] = bank
+
+        def result(c):
+            y = sb(f"y{c}", [P, PACK, CH], F32)
+            if c == 2:
+                nc.vector.tensor_copy(y[:], y_bank[c][:])
+            else:
+                nc.scalar.copy(y[:], y_bank[c][:])
+            nc.sync.dma_start(out_rows[:, :, c * CH : (c + 1) * CH], y[:])
 
         def planes(c):
             yw = sb(f"yw{c}", [P, CH], I32)
@@ -180,30 +187,33 @@ def tile_picked_temper_tanh_po_kernel(
             )
             nc.sync.dma_start(out_words[:, c * CH : (c + 1) * CH], yw[:])
 
-        deal(dsc[:], placed[:, :S])
         queries(0)
         scores(0)
         scores(1)
         queries(1)
         scores(2)
         scores(3)
-        deal(ww[:].bitcast(I32), ww_raw[:])
         temper(0)
-        hidden(0)
-        deal(wsc[:], wsc_raw[:])
-        values(0)
         temper(1)
+        hidden(0)
+        deal(ww[:].bitcast(I32), ww_raw[:])
+        values(0)
         hidden(1)
-        planes(0)
         values(1)
-        hidden(2)
-        values(2)
         temper(2)
-        planes(1)
+        temper(3)
+        hidden(2)
+        result(0)
+        planes(0)
+        values(2)
         hidden(3)
+        result(1)
+        planes(1)
         values(3)
+        result(2)
         planes(2)
         planes(3)
+        result(3)
         for q in range(4):
             eng = nc.sync if q % 2 else nc.scalar
             eng.dma_start(out_2[0, 4 * q : 4 * q + 4, :].bitcast(I32), y_scales[32 * q : 32 * q + 4, :].bitcast(I32))

@@ -45,7 +45,7 @@ def tile_picked_temper_tanh_po_kernel(
         xsc_win = sb("xsc_win", [P, TABLE], U8)
         wsc_raw = sb("wsc_raw", [P, S], U8)
         warm = sb("warm", [P, 1], F32)
-        dw_win = reuse.tile([P, TABLE], I32, name="dw_win", offset=3 * TABLE)
+        dw_win = reuse.tile([P, TABLE], I32, name="dw_win", offset=2 * TABLE)
         xw_win = sb("xw_win", [P, TABLE], I32)
         warm_out = sb("warm_out", [P, 1], F32)
 
@@ -55,27 +55,33 @@ def tile_picked_temper_tanh_po_kernel(
             return rows.unsqueeze(1).to_broadcast([16, 8, rows.shape[1]])
 
         nc.sync.dma_start(kidx_sb[:], kidx)
+        nc.scalar.dma_start(wsc_raw[:].bitcast(I32), spread(w1_scales))
         nc.scalar.dma_start(dsc_win[:].bitcast(I32), spread(d_scales))
         nc.sync.dma_start(offs_sb[:], offs)
         nc.scalar.dma_start(xsc_win[:].bitcast(I32), spread(x_scales))
         nc.sync.dma_start(task_sb[:], task)
-        nc.scalar.dma_start(wsc_raw[:].bitcast(I32), spread(w1_scales))
+        gn_sb = sb("gn_sb", [P, PACK], F32)
+        nc.scalar.dma_start(gn_sb[:], gn.rearrange("(p t) o -> p (t o)", t=PACK))
         nc.sync.dma_start(dw_win[:], words_of(d_words))
         nc.sync.dma_start(xw_win[:], words_of(x_words))
+        temp_rows = temp.rearrange("(p t) u -> p t u", t=PACK)
+        temp_sb = [sb(f"temp{t}", [P, S], F32) for t in range(2)]
+        for t in range(2):
+            nc.sync.dma_start(temp_sb[t][:], temp_rows[:, t, :])
         nc.vector.memset(warm[:], 0.0)
         nc.scalar.activation(warm_out[:], warm[:], ACT.Tanh)
 
         def deal(dst, src):
             nc.vector.tensor_copy(dst.rearrange("p (t m) -> p m t", t=PACK), src.rearrange("p (m t) -> p m t", t=PACK))
 
-        dsc_g = sb("dsc_g", [P, S], U8)
-        nc.vector.tensor_copy(dsc_g[:], dsc_win[:].indirect(kidx_sb[:]))
-        xsc_g = reuse.tile([P, S], U8, name="xsc_g", offset=2 * TABLE - S // 2)
-        nc.vector.tensor_copy(xsc_g[:], xsc_win[:].indirect(offs_sb[:]))
         planes3 = sb("planes3", [P, 3 * S], U8)
         dsc, wsc, xsc = planes3[:, :S], planes3[:, S : 2 * S], planes3[:, 2 * S :]
-        deal(dsc, dsc_g[:])
         deal(wsc, wsc_raw[:])
+        dsc_g = sb("dsc_g", [P, S], U8)
+        nc.vector.tensor_copy(dsc_g[:], dsc_win[:].indirect(kidx_sb[:]))
+        xsc_g = reuse.tile([P, S], U8, name="xsc_g", offset=TABLE - S // 2)
+        nc.vector.tensor_copy(xsc_g[:], xsc_win[:].indirect(offs_sb[:]))
+        deal(dsc, dsc_g[:])
         nc.vector.tensor_copy(xsc.bitcast(I32), xsc_g[:].bitcast(I32))
         for r in range(1, 4):
             nc.sync.dma_start(planes3[r:P:32, :].bitcast(I32), planes3[8 * r : P : 32, :].bitcast(I32))
@@ -83,16 +89,12 @@ def tile_picked_temper_tanh_po_kernel(
         nc.vector.tensor_copy(dw_g[:], dw_win[:].bitcast(U32).indirect(kidx_sb[:]))
         dw = sb("dw", [P, S], U32)
         deal(dw[:].bitcast(I32), dw_g[:].bitcast(I32))
-        temp_rows = temp.rearrange("(p t) u -> p t u", t=PACK)
-        temp_sb = []
-        for t in range(PACK):
-            tt = reuse.tile([P, S], F32, name=f"temp{t}", offset=(t + 1) * TABLE)
-            nc.sync.dma_start(tt[:], temp_rows[:, t, :])
-            temp_sb.append(tt)
-        ww_raw = reuse.tile([P, S], I32, name="ww_raw", offset=5 * TABLE)
+        for t in range(2, PACK):
+            late = reuse.tile([P, S], F32, name=f"temp{t}", offset=(t - 2) * TABLE)
+            nc.sync.dma_start(late[:], temp_rows[:, t, :])
+            temp_sb.append(late)
+        ww_raw = reuse.tile([P, S], I32, name="ww_raw", offset=2 * TABLE)
         nc.sync.dma_start(ww_raw[:], words_of(w1_words))
-        gn_sb = reuse.tile([P, PACK], F32, name="gn_sb", offset=6 * TABLE)
-        nc.sync.dma_start(gn_sb[:], gn.rearrange("(p t) o -> p (t o)", t=PACK))
         xw = [sb(f"xw{h}", [P, GW], U32) for h in range(S // GW)]
 
         def queries(h):
@@ -103,8 +105,11 @@ def tile_picked_temper_tanh_po_kernel(
         out_rows = out_0.rearrange("(p t) j -> p t j", t=PACK)
         out_words = words_of(out_1)
         per = GW // CH
-        s_sb = {}
+        s_mid = sb("s_mid", [P, PACK, 2 * CH], F32)
+        s_last = ring.tile([P, PACK, CH], F32, name="s_last", offset=4 * TABLE, align_bytes=64)
+        s_sb = {1: s_mid, 3: s_last}
         u_sb = {}
+        yw = sb("yw", [P, S], I32)
         zq = {}
         y_bank = {}
 
@@ -122,33 +127,42 @@ def tile_picked_temper_tanh_po_kernel(
                     stop=True,
                 )
             if c == 0:
-                s_sb[c] = bank
+                y_bank["s0"] = bank
                 return
-            s_sb[c] = sb(f"s{c}", [P, PACK, CH], F32)
-            nc.scalar.copy(s_sb[c][:], bank[:])
+            nc.scalar.copy(s_last[:] if c == 3 else s_mid[:, :, (c - 1) * CH : c * CH], bank[:])
 
-        def temper(c):
-            u_sb[c] = ring.tile([P, PACK, CH], F32, name=f"u{c}", tag=f"slot{c}", align_bytes=64)
-            if c == 0:
-                tg = ring.tile([P, PACK, CH], F32, name="tg", tag="slot1", align_bytes=64)
-                for t in range(PACK):
-                    nc.vector.tensor_copy(tg[:, t, :], temp_sb[t][:].indirect(task_sb[:, : CH // 16]))
-                nc.vector.tensor_tensor(u_sb[c][:], s_sb[c][:], tg[:], MULT)
-                return
+        def temper_first():
+            u = ring.tile([P, PACK, CH], F32, name="u_first", offset=0, align_bytes=64)
+            tg = ring.tile([P, PACK, CH], F32, name="tg", offset=TABLE, align_bytes=64)
+            for t in range(PACK):
+                nc.vector.tensor_copy(tg[:, t, :], temp_sb[t][:].indirect(task_sb[:, : CH // 16]))
+            nc.vector.tensor_tensor(u[:], y_bank["s0"][:], tg[:], MULT)
+            u_sb[0] = u[:]
+
+        def temper(first, count):
+            lo, width = first * CH, count * CH
+            u = ring.tile([P, PACK, width], F32, name=f"u{first}", offset=first * TABLE, align_bytes=64)
             for t in range(PACK):
                 nc.vector.tensor_tensor(
-                    u_sb[c][:, t, :], temp_sb[t][:].indirect(task_sb[:, c * CH // 16 : (c + 1) * CH // 16]), s_sb[c][:, t, :], MULT
+                    u[:, t, :], temp_sb[t][:].indirect(task_sb[:, lo // 16 : (lo + width) // 16]), s_sb[first][:, t, :], MULT
                 )
+            for i in range(count):
+                u_sb[first + i] = u[:, :, i * CH : (i + 1) * CH]
 
         def hidden(c):
             th = sb(f"th{c}", [P, CH, PACK], F32)
             nc.scalar.activation(
                 th[:].rearrange("p (c i) t -> p c t i", i=4),
-                u_sb[c][:].rearrange("p t (c i) -> p c t i", i=4),
+                u_sb[c].rearrange("p t (c i) -> p c t i", i=4),
                 ACT.Tanh,
                 scale=0.0625,
             )
-            zb = ring.tile([P, CH, PACK], BF16, name=f"zb{c}", tag=f"slot{c + 2}", align_bytes=64)
+            if c == 0:
+                zb = ring.tile([P, CH, PACK], BF16, name="zb0", offset=3 * TABLE, align_bytes=64)
+            elif c == 1:
+                zb = ring.tile([P, CH, PACK], BF16, name="zb1", offset=4 * TABLE, align_bytes=64)
+            else:
+                zb = sb(f"zb{c}", [P, CH, PACK], BF16)
             nc.vector.tensor_tensor(zb[:], th[:], gn_sb[:].unsqueeze(1).to_broadcast([P, CH, PACK]), MULT)
             zq[c] = zb
 
@@ -167,25 +181,30 @@ def tile_picked_temper_tanh_po_kernel(
                     start=True,
                     stop=True,
                 )
-            yb = sb(f"yb{c}", [P, CH, PACK], BF16)
-            nc.scalar.copy(yb[:], bank[:].rearrange("p t j -> p j t"))
-            zq[c] = yb
-            y_bank[c] = bank
-
-        def result(c):
             y = sb(f"y{c}", [P, PACK, CH], F32)
-            if c == 2:
-                nc.vector.tensor_copy(y[:], y_bank[c][:])
+            nc.scalar.copy(y[:], bank[:])
+            eng = nc.scalar if c == 3 else nc.sync
+            eng.dma_start(out_rows[:, :, c * CH : (c + 1) * CH], y[:])
+            y_bank[c] = (bank, y)
+
+        def rounded(c):
+            bank, y = y_bank[c]
+            yb = sb(f"yb{c}", [P, CH, PACK], BF16)
+            if c == 0:
+                nc.scalar.copy(yb[:], bank[:].rearrange("p t j -> p j t"))
             else:
-                nc.scalar.copy(y[:], y_bank[c][:])
-            nc.sync.dma_start(out_rows[:, :, c * CH : (c + 1) * CH], y[:])
+                nc.vector.tensor_copy(
+                    yb[:].rearrange("p (c i) t -> p c t i", i=4), y[:].rearrange("p t (c i) -> p c t i", i=4)
+                )
+            zq[c] = yb
 
         def planes(c):
-            yw = sb(f"yw{c}", [P, CH], I32)
             nc.vector.quantize_mx(
-                out=yw[:].bitcast(FP8X4), scales=y_scales[:, c * CH : (c + 1) * CH], in_=zq[c][:].rearrange("p j t -> p (j t)")
+                out=yw[:, c * CH : (c + 1) * CH].bitcast(FP8X4), scales=y_scales[:, c * CH : (c + 1) * CH], in_=zq[c][:].rearrange("p j t -> p (j t)")
             )
-            nc.sync.dma_start(out_words[:, c * CH : (c + 1) * CH], yw[:])
+            if c % 2:
+                lo = (c - 1) * CH
+                nc.sync.dma_start(out_words[:, lo : (c + 1) * CH], yw[:, lo : (c + 1) * CH])
 
         queries(0)
         scores(0)
@@ -193,27 +212,22 @@ def tile_picked_temper_tanh_po_kernel(
         queries(1)
         scores(2)
         scores(3)
-        temper(0)
-        temper(1)
-        hidden(0)
+        temper_first()
         deal(ww[:].bitcast(I32), ww_raw[:])
+        temper(1, 2)
+        hidden(0)
         values(0)
+        rounded(0)
+        temper(3, 1)
         hidden(1)
-        values(1)
-        temper(2)
-        temper(3)
         hidden(2)
-        result(0)
-        planes(0)
-        values(2)
+        values(1)
         hidden(3)
-        result(1)
-        planes(1)
+        values(2)
         values(3)
-        result(2)
-        planes(2)
-        planes(3)
-        result(3)
+        planes(0)
+        for c in range(1, S // CH):
+            rounded(c)
+            planes(c)
         for q in range(4):
-            eng = nc.sync if q % 2 else nc.scalar
-            eng.dma_start(out_2[0, 4 * q : 4 * q + 4, :].bitcast(I32), y_scales[32 * q : 32 * q + 4, :].bitcast(I32))
+            nc.sync.dma_start(out_2[0, 4 * q : 4 * q + 4, :].bitcast(I32), y_scales[32 * q : 32 * q + 4, :].bitcast(I32))

@@ -71,17 +71,22 @@ def tile_picked_temper_tanh_po_kernel(
         nc.vector.memset(warm[:], 0.0)
         nc.scalar.activation(warm_out[:], warm[:], ACT.Tanh)
 
+        def deal_bytes(dst, src):
+            nc.vector.tensor_copy(dst.rearrange("p (t m) -> p t m", t=PACK), src.rearrange("p (m t) -> p t m", t=PACK))
+
         def deal(dst, src):
-            nc.vector.tensor_copy(dst.rearrange("p (t m) -> p m t", t=PACK), src.rearrange("p (m t) -> p m t", t=PACK))
+            nc.vector.tensor_copy(
+                dst.rearrange("p (t c i) -> p c t i", t=PACK, i=4), src.rearrange("p (c i t) -> p c t i", t=PACK, i=4)
+            )
 
         planes3 = sb("planes3", [P, 3 * S], U8)
         dsc, wsc, xsc = planes3[:, :S], planes3[:, S : 2 * S], planes3[:, 2 * S :]
-        deal(wsc, wsc_raw[:])
+        deal_bytes(wsc, wsc_raw[:])
         dsc_g = sb("dsc_g", [P, S], U8)
         nc.vector.tensor_copy(dsc_g[:], dsc_win[:].indirect(kidx_sb[:]))
         xsc_g = reuse.tile([P, S], U8, name="xsc_g", offset=TABLE - S // 2)
         nc.vector.tensor_copy(xsc_g[:], xsc_win[:].indirect(offs_sb[:]))
-        deal(dsc, dsc_g[:])
+        deal_bytes(dsc, dsc_g[:])
         nc.vector.tensor_copy(xsc.bitcast(I32), xsc_g[:].bitcast(I32))
         for r in range(1, 4):
             nc.sync.dma_start(planes3[r:P:32, :].bitcast(I32), planes3[8 * r : P : 32, :].bitcast(I32))
@@ -95,48 +100,64 @@ def tile_picked_temper_tanh_po_kernel(
             temp_sb.append(late)
         ww_raw = reuse.tile([P, S], I32, name="ww_raw", offset=2 * TABLE)
         nc.sync.dma_start(ww_raw[:], words_of(w1_words))
-        xw = [sb(f"xw{h}", [P, GW], U32) for h in range(S // GW)]
+        xw = sb("xw", [P, S], U32)
 
         def queries(h):
-            nc.vector.tensor_copy(xw[h][:], xw_win[:].bitcast(U32).indirect(offs_sb[:, h * GW // 16 : (h + 1) * GW // 16]))
+            nc.vector.tensor_copy(xw[:, h * GW : (h + 1) * GW], xw_win[:].bitcast(U32).indirect(offs_sb[:, h * GW // 16 : (h + 1) * GW // 16]))
 
         ww = sb("ww", [P, S], U32)
         y_scales = sb("y_scales", [P, S], U8)
         out_rows = out_0.rearrange("(p t) j -> p t j", t=PACK)
         out_words = words_of(out_1)
-        per = GW // CH
         s_mid = sb("s_mid", [P, PACK, 2 * CH], F32)
-        s_last = ring.tile([P, PACK, CH], F32, name="s_last", offset=4 * TABLE, align_bytes=64)
+        s_last = ring.tile([P, PACK, CH], F32, name="s_last", offset=7 * TABLE, align_bytes=64)
         s_sb = {1: s_mid, 3: s_last}
         u_sb = {}
-        yw = sb("yw", [P, S], I32)
+        s_side = sb("s_side", [P, CH], F32)
+        yw = ring.tile([P, S], I32, name="yw", offset=5 * TABLE, align_bytes=64)
         zq = {}
         y_bank = {}
 
-        def scores(c):
-            h, lo = c // per, (c % per) * CH
-            bank = psum.tile([P, PACK, CH], F32, name=f"s_bank{c}")
+        def score(out, t, lo, hi):
+            nc.tensor.matmul_mx(
+                out=out,
+                lhsT=dw[:, t * P : (t + 1) * P].bitcast(FP8X4),
+                lhsT_scale=dsc[:, t * P : (t + 1) * P],
+                rhs=xw[:, lo:hi].bitcast(FP8X4),
+                rhs_scale=xsc[:, lo:hi],
+                start=True,
+                stop=True,
+            )
+
+        def scores_first():
+            side = psum.tile([P, CH], F32, name="y_bank3")
+            score(side[:], 3, 0, CH)
+            nc.scalar.copy(s_side[:], side[:])
+            bank = psum.tile([P, 3, CH], F32, name="s_bank0")
+            for t in range(3):
+                score(bank[:, t, :], t, 0, CH)
+            y_bank["s0"] = bank
+
+        def scores_mid():
+            for pair in range(2):
+                bank = psum.tile([P, 2, 2 * CH], F32, name=f"s_bank{1 + pair}")
+                for e in range(2):
+                    score(bank[:, e, :], 2 * pair + e, CH, 3 * CH)
+                nc.scalar.copy(s_mid[:, 2 * pair : 2 * pair + 2, :], bank[:])
+
+        def scores_last():
+            bank = psum.tile([P, PACK, CH], F32, name="s_bank3")
             for t in range(PACK):
-                nc.tensor.matmul_mx(
-                    out=bank[:, t, :],
-                    lhsT=dw[:, t * P : (t + 1) * P].bitcast(FP8X4),
-                    lhsT_scale=dsc[:, t * P : (t + 1) * P],
-                    rhs=xw[h][:, lo : lo + CH].bitcast(FP8X4),
-                    rhs_scale=xsc[:, c * CH : (c + 1) * CH],
-                    start=True,
-                    stop=True,
-                )
-            if c == 0:
-                y_bank["s0"] = bank
-                return
-            nc.scalar.copy(s_last[:] if c == 3 else s_mid[:, :, (c - 1) * CH : c * CH], bank[:])
+                score(bank[:, t, :], t, 3 * CH, S)
+            y_bank["s3"] = bank
 
         def temper_first():
             u = ring.tile([P, PACK, CH], F32, name="u_first", offset=0, align_bytes=64)
-            tg = ring.tile([P, PACK, CH], F32, name="tg", offset=TABLE, align_bytes=64)
-            for t in range(PACK):
+            tg = ring.tile([P, 3, CH], F32, name="tg", offset=TABLE, align_bytes=64)
+            for t in range(3):
                 nc.vector.tensor_copy(tg[:, t, :], temp_sb[t][:].indirect(task_sb[:, : CH // 16]))
-            nc.vector.tensor_tensor(u[:], y_bank["s0"][:], tg[:], MULT)
+            nc.vector.tensor_tensor(u[:, 3, :], temp_sb[3][:].indirect(task_sb[:, : CH // 16]), s_side[:], MULT)
+            nc.vector.tensor_tensor(u[:, :3, :], y_bank["s0"][:], tg[:], MULT)
             u_sb[0] = u[:]
 
         def temper(first, count):
@@ -149,85 +170,116 @@ def tile_picked_temper_tanh_po_kernel(
             for i in range(count):
                 u_sb[first + i] = u[:, :, i * CH : (i + 1) * CH]
 
-        def hidden(c):
-            th = sb(f"th{c}", [P, CH, PACK], F32)
+        def hidden_first():
+            th = sb("th0", [P, PACK, CH], F32)
+            nc.scalar.activation(th[:], u_sb[0], ACT.Tanh, scale=0.0625)
+            zp = ring.tile([P, PACK, CH], BF16, name="zp0", offset=4 * TABLE, align_bytes=64)
+            for t in range(PACK):
+                nc.scalar.activation(zp[:, t, :], th[:, t, :], ACT.Copy, scale=gn_sb[:, t : t + 1])
+            zb = sb("zb0", [P, CH, PACK], BF16)
+            nc.scalar.copy(zb[:].rearrange("p (c i) t -> p c t i", i=4), zp[:].rearrange("p t (c i) -> p c t i", i=4))
+            zq[0] = zb
+
+        th_sb = {}
+        th_mid = ring.tile([P, 3 * CH, PACK], F32, name="th_mid", offset=4 * TABLE, align_bytes=64)
+
+        def squash(c):
+            th = th_mid[:, (c - 1) * CH : c * CH, :]
             nc.scalar.activation(
-                th[:].rearrange("p (c i) t -> p c t i", i=4),
+                th.rearrange("p (c i) t -> p c t i", i=4),
                 u_sb[c].rearrange("p t (c i) -> p c t i", i=4),
                 ACT.Tanh,
                 scale=0.0625,
             )
-            if c == 0:
-                zb = ring.tile([P, CH, PACK], BF16, name="zb0", offset=3 * TABLE, align_bytes=64)
-            elif c == 1:
-                zb = ring.tile([P, CH, PACK], BF16, name="zb1", offset=4 * TABLE, align_bytes=64)
-            else:
-                zb = sb(f"zb{c}", [P, CH, PACK], BF16)
-            nc.vector.tensor_tensor(zb[:], th[:], gn_sb[:].unsqueeze(1).to_broadcast([P, CH, PACK]), MULT)
+            th_sb[c] = th
+
+        def gain(c):
+            zb = sb(f"zb{c}", [P, CH, PACK], BF16)
+            nc.vector.tensor_tensor(zb[:], th_sb[c], gn_sb[:].unsqueeze(1).to_broadcast([P, CH, PACK]), MULT)
             zq[c] = zb
 
+        y_sb = {}
+
         def values(c):
-            zw = sb(f"zw{c}", [P, CH], U32)
+            if c in (1, 2):
+                zw = ring.tile([P, CH], U32, name=f"zw{c}", offset=(c + 1) * TABLE, align_bytes=64)
+            else:
+                zw = sb(f"zw{c}", [P, CH], U32)
             zs = sb(f"zs{c}", [P, CH], U8)
             nc.vector.quantize_mx(out=zw[:].bitcast(FP8X4), scales=zs[:], in_=zq[c][:].rearrange("p j t -> p (j t)"))
-            bank = psum.tile([P, PACK, CH], F32, name=f"y_bank{c}")
-            for t in range(PACK):
-                nc.tensor.matmul_mx(
-                    out=bank[:, t, :],
-                    lhsT=ww[:, t * P : (t + 1) * P].bitcast(FP8X4),
-                    lhsT_scale=wsc[:, t * P : (t + 1) * P],
-                    rhs=zw[:].bitcast(FP8X4),
-                    rhs_scale=zs[:],
-                    start=True,
-                    stop=True,
-                )
+            groups = [(0, 2, "y_bank3"), (2, 4, "s_bank0")] if c == 3 else [(0, 4, f"y_bank{c}")]
+            banks = []
+            for lo, hi, tag in groups:
+                bank = psum.tile([P, hi - lo, CH], F32, name=tag)
+                for t in range(lo, hi):
+                    nc.tensor.matmul_mx(
+                        out=bank[:, t - lo, :],
+                        lhsT=ww[:, t * P : (t + 1) * P].bitcast(FP8X4),
+                        lhsT_scale=wsc[:, t * P : (t + 1) * P],
+                        rhs=zw[:].bitcast(FP8X4),
+                        rhs_scale=zs[:],
+                        start=True,
+                        stop=True,
+                    )
+                banks.append((lo, hi, bank))
+            y_bank[c] = banks
+
+        def result(c):
             y = sb(f"y{c}", [P, PACK, CH], F32)
-            nc.scalar.copy(y[:], bank[:])
-            eng = nc.scalar if c == 3 else nc.sync
-            eng.dma_start(out_rows[:, :, c * CH : (c + 1) * CH], y[:])
-            y_bank[c] = (bank, y)
+            for lo, hi, bank in y_bank[c]:
+                nc.scalar.copy(y[:, lo:hi, :], bank[:])
+            nc.sync.dma_start(out_rows[:, :, c * CH : (c + 1) * CH], y[:])
+            y_sb[c] = y
+
+        yb_sb = {}
 
         def rounded(c):
-            bank, y = y_bank[c]
             yb = sb(f"yb{c}", [P, CH, PACK], BF16)
             if c == 0:
-                nc.scalar.copy(yb[:], bank[:].rearrange("p t j -> p j t"))
+                nc.scalar.copy(yb[:], y_bank[c][0][2][:].rearrange("p t j -> p j t"))
             else:
                 nc.vector.tensor_copy(
-                    yb[:].rearrange("p (c i) t -> p c t i", i=4), y[:].rearrange("p t (c i) -> p c t i", i=4)
+                    yb[:].rearrange("p (c i) t -> p c t i", i=4), y_sb[c][:].rearrange("p t (c i) -> p c t i", i=4)
                 )
-            zq[c] = yb
+            yb_sb[c] = yb
 
         def planes(c):
             nc.vector.quantize_mx(
-                out=yw[:, c * CH : (c + 1) * CH].bitcast(FP8X4), scales=y_scales[:, c * CH : (c + 1) * CH], in_=zq[c][:].rearrange("p j t -> p (j t)")
+                out=yw[:, c * CH : (c + 1) * CH].bitcast(FP8X4), scales=y_scales[:, c * CH : (c + 1) * CH], in_=yb_sb[c][:].rearrange("p j t -> p (j t)")
             )
-            if c % 2:
-                lo = (c - 1) * CH
+            if c >= 2:
+                lo = 0 if c == 2 else c * CH
                 nc.sync.dma_start(out_words[:, lo : (c + 1) * CH], yw[:, lo : (c + 1) * CH])
 
         queries(0)
-        scores(0)
-        scores(1)
+        scores_first()
         queries(1)
-        scores(2)
-        scores(3)
+        scores_mid()
+        scores_last()
         temper_first()
         deal(ww[:].bitcast(I32), ww_raw[:])
         temper(1, 2)
-        hidden(0)
-        values(0)
-        rounded(0)
+        hidden_first()
+        nc.scalar.copy(s_last[:], y_bank["s3"][:])
         temper(3, 1)
-        hidden(1)
-        hidden(2)
+        values(0)
+        squash(1)
+        squash(2)
+        squash(3)
+        result(0)
+        rounded(0)
+        gain(1)
+        gain(2)
         values(1)
-        hidden(3)
+        gain(3)
         values(2)
         values(3)
         planes(0)
         for c in range(1, S // CH):
+            result(c)
+        for c in range(1, S // CH):
             rounded(c)
             planes(c)
         for q in range(4):
-            nc.sync.dma_start(out_2[0, 4 * q : 4 * q + 4, :].bitcast(I32), y_scales[32 * q : 32 * q + 4, :].bitcast(I32))
+            eng = nc.scalar if q % 2 else nc.sync
+            eng.dma_start(out_2[0, 4 * q : 4 * q + 4, :].bitcast(I32), y_scales[32 * q : 32 * q + 4, :].bitcast(I32))

@@ -45,7 +45,7 @@ def tile_picked_temper_tanh_po_kernel(
         xsc_win = sb("xsc_win", [P, TABLE], U8)
         wsc_raw = sb("wsc_raw", [P, S], U8)
         warm = sb("warm", [P, 1], F32)
-        dw_win = reuse.tile([P, TABLE], I32, name="dw_win", offset=2 * TABLE)
+        dw_win = reuse.tile([P, TABLE], I32, name="dw_win", offset=3 * TABLE)
         xw_win = sb("xw_win", [P, TABLE], I32)
         warm_out = sb("warm_out", [P, 1], F32)
 
@@ -65,8 +65,8 @@ def tile_picked_temper_tanh_po_kernel(
         nc.sync.dma_start(dw_win[:], words_of(d_words))
         nc.sync.dma_start(xw_win[:], words_of(x_words))
         temp_rows = temp.rearrange("(p t) u -> p t u", t=PACK)
-        temp_sb = [sb(f"temp{t}", [P, S], F32) for t in range(2)]
-        for t in range(2):
+        temp_sb = [sb(f"temp{t}", [P, S], F32) for t in range(1)]
+        for t in range(1):
             nc.sync.dma_start(temp_sb[t][:], temp_rows[:, t, :])
         nc.vector.memset(warm[:], 0.0)
         nc.scalar.activation(warm_out[:], warm[:], ACT.Tanh)
@@ -83,22 +83,37 @@ def tile_picked_temper_tanh_po_kernel(
         dsc, wsc, xsc = planes3[:, :S], planes3[:, S : 2 * S], planes3[:, 2 * S :]
         deal_bytes(wsc, wsc_raw[:])
         dsc_g = sb("dsc_g", [P, S], U8)
-        nc.vector.tensor_copy(dsc_g[:], dsc_win[:].indirect(kidx_sb[:]))
-        xsc_g = reuse.tile([P, S], U8, name="xsc_g", offset=TABLE - S // 2)
-        nc.vector.tensor_copy(xsc_g[:], xsc_win[:].indirect(offs_sb[:]))
-        deal_bytes(dsc, dsc_g[:])
-        nc.vector.tensor_copy(xsc.bitcast(I32), xsc_g[:].bitcast(I32))
+        for h in range(2):
+            nc.vector.tensor_copy(dsc_g[:, h * GW : (h + 1) * GW], dsc_win[:].indirect(kidx_sb[:, h * GW // 16 : (h + 1) * GW // 16]))
+
+        def deal_half(h):
+            nc.vector.tensor_copy(
+                dsc.rearrange("p (t h m) -> p h t m", t=PACK, h=2)[:, h], dsc_g[:].rearrange("p (h m t) -> p h t m", t=PACK, h=2)[:, h]
+            )
+
+        deal_half(0)
+        xsc_g = reuse.tile([P, TABLE + S], U8, name="xsc_g", offset=TABLE - S // 2)[:, :S]
+        nc.vector.tensor_copy(xsc_g, xsc_win[:].indirect(offs_sb[:]))
+        deal_half(1)
+        nc.vector.tensor_copy(xsc.bitcast(I32), xsc_g.bitcast(I32))
         for r in range(1, 4):
             nc.sync.dma_start(planes3[r:P:32, :].bitcast(I32), planes3[8 * r : P : 32, :].bitcast(I32))
         dw_g = sb("dw_g", [P, S], U32)
-        nc.vector.tensor_copy(dw_g[:], dw_win[:].bitcast(U32).indirect(kidx_sb[:]))
         dw = sb("dw", [P, S], U32)
-        deal(dw[:].bitcast(I32), dw_g[:].bitcast(I32))
-        for t in range(2, PACK):
-            late = reuse.tile([P, S], F32, name=f"temp{t}", offset=(t - 2) * TABLE)
+        for h in range(2):
+            nc.vector.tensor_copy(
+                dw_g[:, h * GW : (h + 1) * GW], dw_win[:].bitcast(U32).indirect(kidx_sb[:, h * GW // 16 : (h + 1) * GW // 16])
+            )
+        for h in range(2):
+            nc.vector.tensor_copy(
+                dw[:].bitcast(I32).rearrange("p (t h c i) -> p h c t i", t=PACK, h=2, i=4)[:, h],
+                dw_g[:].bitcast(I32).rearrange("p (h c i t) -> p h c t i", t=PACK, h=2, i=4)[:, h],
+            )
+        for t in range(1, PACK):
+            late = reuse.tile([P, S], F32, name=f"temp{t}", offset=(t - 1) * TABLE)
             nc.sync.dma_start(late[:], temp_rows[:, t, :])
             temp_sb.append(late)
-        ww_raw = reuse.tile([P, S], I32, name="ww_raw", offset=2 * TABLE)
+        ww_raw = reuse.tile([P, S], I32, name="ww_raw", offset=3 * TABLE)
         nc.sync.dma_start(ww_raw[:], words_of(w1_words))
         xw = sb("xw", [P, S], U32)
 
@@ -247,8 +262,8 @@ def tile_picked_temper_tanh_po_kernel(
             nc.vector.quantize_mx(
                 out=yw[:, c * CH : (c + 1) * CH].bitcast(FP8X4), scales=y_scales[:, c * CH : (c + 1) * CH], in_=yb_sb[c][:].rearrange("p j t -> p (j t)")
             )
-            if c >= 2:
-                lo = 0 if c == 2 else c * CH
+            if c != 1:
+                lo = CH if c == 2 else c * CH
                 nc.sync.dma_start(out_words[:, lo : (c + 1) * CH], yw[:, lo : (c + 1) * CH])
 
         queries(0)

@@ -54,8 +54,8 @@ def tile_picked_temper_tanh_po_kernel(
             rows = scales[0].bitcast(I32)
             return rows.unsqueeze(1).to_broadcast([16, 8, rows.shape[1]])
 
+        nc.sync.dma_start(wsc_raw[:].bitcast(I32), spread(w1_scales))
         nc.sync.dma_start(kidx_sb[:], kidx)
-        nc.scalar.dma_start(wsc_raw[:].bitcast(I32), spread(w1_scales))
         nc.scalar.dma_start(dsc_win[:].bitcast(I32), spread(d_scales))
         nc.sync.dma_start(offs_sb[:], offs)
         nc.scalar.dma_start(xsc_win[:].bitcast(I32), spread(x_scales))
@@ -91,9 +91,9 @@ def tile_picked_temper_tanh_po_kernel(
                 dsc.rearrange("p (t h m) -> p h t m", t=PACK, h=2)[:, h], dsc_g[:].rearrange("p (h m t) -> p h t m", t=PACK, h=2)[:, h]
             )
 
-        deal_half(0)
         xsc_g = reuse.tile([P, TABLE + S], U8, name="xsc_g", offset=TABLE - S // 2)[:, :S]
         nc.vector.tensor_copy(xsc_g, xsc_win[:].indirect(offs_sb[:]))
+        deal_half(0)
         deal_half(1)
         nc.vector.tensor_copy(xsc.bitcast(I32), xsc_g.bitcast(I32))
         for r in range(1, 4):
@@ -187,9 +187,10 @@ def tile_picked_temper_tanh_po_kernel(
 
         def hidden_first():
             th = sb("th0", [P, PACK, CH], F32)
-            nc.scalar.activation(th[:], u_sb[0], ACT.Tanh, scale=0.0625)
+            nc.scalar.activation(th[:, 3, :], u_sb[0][:, 3, :], ACT.Tanh, scale=0.0625)
+            nc.scalar.activation(th[:, :3, :], u_sb[0][:, :3, :], ACT.Tanh, scale=0.0625)
             zp = ring.tile([P, PACK, CH], BF16, name="zp0", offset=4 * TABLE, align_bytes=64)
-            for t in range(PACK):
+            for t in (3, 0, 1, 2):
                 nc.scalar.activation(zp[:, t, :], th[:, t, :], ACT.Copy, scale=gn_sb[:, t : t + 1])
             zb = sb("zb0", [P, CH, PACK], BF16)
             nc.scalar.copy(zb[:].rearrange("p (c i) t -> p c t i", i=4), zp[:].rearrange("p t (c i) -> p c t i", i=4))

@@ -54,14 +54,15 @@ def tile_picked_temper_tanh_po_kernel(
             rows = scales[0].bitcast(I32)
             return rows.unsqueeze(1).to_broadcast([16, 8, rows.shape[1]])
 
-        nc.sync.dma_start(wsc_raw[:].bitcast(I32), spread(w1_scales))
+        for win in (dsc_win, xsc_win):
+            nc.vector.memset(win[:].bitcast(I32)[:, :GW], 0)
+            nc.gpsimd.memset(win[:].bitcast(I32)[:, GW:], 0)
         nc.sync.dma_start(kidx_sb[:], kidx)
-        nc.scalar.dma_start(dsc_win[:].bitcast(I32), spread(d_scales))
+        nc.scalar.dma_start(wsc_raw[:].bitcast(I32), spread(w1_scales))
         nc.sync.dma_start(offs_sb[:], offs)
-        nc.scalar.dma_start(xsc_win[:].bitcast(I32), spread(x_scales))
+        nc.sync.dma_start(dsc_win[0:P:8, :].bitcast(I32), d_scales[0].bitcast(I32))
         nc.sync.dma_start(task_sb[:], task)
-        gn_sb = sb("gn_sb", [P, PACK], F32)
-        nc.scalar.dma_start(gn_sb[:], gn.rearrange("(p t) o -> p (t o)", t=PACK))
+        nc.sync.dma_start(xsc_win[0:P:8, :].bitcast(I32), x_scales[0].bitcast(I32))
         nc.sync.dma_start(dw_win[:], words_of(d_words))
         nc.sync.dma_start(xw_win[:], words_of(x_words))
         temp_rows = temp.rearrange("(p t) u -> p t u", t=PACK)
@@ -115,6 +116,8 @@ def tile_picked_temper_tanh_po_kernel(
             temp_sb.append(late)
         ww_raw = reuse.tile([P, S], I32, name="ww_raw", offset=3 * TABLE)
         nc.sync.dma_start(ww_raw[:], words_of(w1_words))
+        gn_sb = reuse.tile([P, PACK], F32, name="gn_sb", offset=4 * TABLE)
+        nc.sync.dma_start(gn_sb[:], gn.rearrange("(p t) o -> p (t o)", t=PACK))
         xw = sb("xw", [P, S], U32)
 
         def queries(h):

@@ -50,15 +50,12 @@ def tile_picked_temper_tanh_po_kernel(
         warm_out = sb("warm_out", [P, 1], F32)
 
 
-        def spread(scales):
-            rows = scales[0].bitcast(I32)
-            return rows.unsqueeze(1).to_broadcast([16, 8, rows.shape[1]])
-
+        nc.gpsimd.memset(wsc_raw[:].bitcast(I32), 0)
         for win in (dsc_win, xsc_win):
-            nc.vector.memset(win[:].bitcast(I32)[:, :GW], 0)
-            nc.gpsimd.memset(win[:].bitcast(I32)[:, GW:], 0)
+            nc.vector.memset(win[:].bitcast(I32)[:, :320], 0)
+            nc.gpsimd.memset(win[:].bitcast(I32)[:, 320:], 0)
         nc.sync.dma_start(kidx_sb[:], kidx)
-        nc.scalar.dma_start(wsc_raw[:].bitcast(I32), spread(w1_scales))
+        nc.scalar.dma_start(wsc_raw[0:P:8, :].bitcast(I32), w1_scales[0].bitcast(I32))
         nc.sync.dma_start(offs_sb[:], offs)
         nc.sync.dma_start(dsc_win[0:P:8, :].bitcast(I32), d_scales[0].bitcast(I32))
         nc.sync.dma_start(task_sb[:], task)
@@ -98,7 +95,7 @@ def tile_picked_temper_tanh_po_kernel(
         deal_half(1)
         nc.vector.tensor_copy(xsc.bitcast(I32), xsc_g.bitcast(I32))
         for r in range(1, 4):
-            nc.sync.dma_start(planes3[r:P:32, :].bitcast(I32), planes3[8 * r : P : 32, :].bitcast(I32))
+            (nc.scalar if r == 2 else nc.sync).dma_start(planes3[r:P:32, :].bitcast(I32), planes3[8 * r : P : 32, :].bitcast(I32))
         dw_g = sb("dw_g", [P, S], U32)
         dw = sb("dw", [P, S], U32)
         for h in range(2):

@@ -45,15 +45,14 @@ def tile_picked_temper_tanh_po_kernel(
         xsc_win = sb("xsc_win", [P, TABLE], U8)
         wsc_raw = sb("wsc_raw", [P, S], U8)
         warm = sb("warm", [P, 1], F32)
-        dw_win = reuse.tile([P, TABLE], I32, name="dw_win", offset=3 * TABLE)
-        xw_win = sb("xw_win", [P, TABLE], I32)
+        dw_win = reuse.tile([P, TABLE], I32, name="dw_win", offset=4 * TABLE)
+        xw_win = reuse.tile([P, TABLE], I32, name="xw_win", offset=8 * TABLE, align_bytes=64)
+        ww_raw = sb("ww_raw", [P, S], I32)
         warm_out = sb("warm_out", [P, 1], F32)
 
 
-        nc.gpsimd.memset(wsc_raw[:].bitcast(I32), 0)
-        for win in (dsc_win, xsc_win):
-            nc.vector.memset(win[:].bitcast(I32)[:, :320], 0)
-            nc.gpsimd.memset(win[:].bitcast(I32)[:, 320:], 0)
+        for win in (wsc_raw, dsc_win, xsc_win):
+            nc.vector.memset(win[:].bitcast(I32), 0)
         nc.sync.dma_start(kidx_sb[:], kidx)
         nc.scalar.dma_start(wsc_raw[0:P:8, :].bitcast(I32), w1_scales[0].bitcast(I32))
         nc.sync.dma_start(offs_sb[:], offs)
@@ -62,10 +61,9 @@ def tile_picked_temper_tanh_po_kernel(
         nc.sync.dma_start(xsc_win[0:P:8, :].bitcast(I32), x_scales[0].bitcast(I32))
         nc.sync.dma_start(dw_win[:], words_of(d_words))
         nc.sync.dma_start(xw_win[:], words_of(x_words))
+        nc.sync.dma_start(ww_raw[:], words_of(w1_words))
         temp_rows = temp.rearrange("(p t) u -> p t u", t=PACK)
-        temp_sb = [sb(f"temp{t}", [P, S], F32) for t in range(1)]
-        for t in range(1):
-            nc.sync.dma_start(temp_sb[t][:], temp_rows[:, t, :])
+        temp_sb = []
         nc.vector.memset(warm[:], 0.0)
         nc.scalar.activation(warm_out[:], warm[:], ACT.Tanh)
 
@@ -89,7 +87,7 @@ def tile_picked_temper_tanh_po_kernel(
                 dsc.rearrange("p (t h m) -> p h t m", t=PACK, h=2)[:, h], dsc_g[:].rearrange("p (h m t) -> p h t m", t=PACK, h=2)[:, h]
             )
 
-        xsc_g = reuse.tile([P, TABLE + S], U8, name="xsc_g", offset=TABLE - S // 2)[:, :S]
+        xsc_g = reuse.tile([P, 2 * TABLE + S], U8, name="xsc_g", offset=TABLE - S // 2)[:, :S]
         nc.vector.tensor_copy(xsc_g, xsc_win[:].indirect(offs_sb[:]))
         deal_half(0)
         deal_half(1)
@@ -107,28 +105,25 @@ def tile_picked_temper_tanh_po_kernel(
                 dw[:].bitcast(I32).rearrange("p (t h c i) -> p h c t i", t=PACK, h=2, i=4)[:, h],
                 dw_g[:].bitcast(I32).rearrange("p (h c i t) -> p h c t i", t=PACK, h=2, i=4)[:, h],
             )
-        for t in range(1, PACK):
-            late = reuse.tile([P, S], F32, name=f"temp{t}", offset=(t - 1) * TABLE)
+        for t in range(PACK):
+            late = reuse.tile([P, S], F32, name=f"temp{t}", offset=t * TABLE)
             nc.sync.dma_start(late[:], temp_rows[:, t, :])
             temp_sb.append(late)
-        ww_raw = reuse.tile([P, S], I32, name="ww_raw", offset=3 * TABLE)
-        nc.sync.dma_start(ww_raw[:], words_of(w1_words))
-        gn_sb = reuse.tile([P, PACK], F32, name="gn_sb", offset=4 * TABLE)
+        gn_sb = reuse.tile([P, PACK], F32, name="gn_sb", offset=5 * TABLE)
         nc.sync.dma_start(gn_sb[:], gn.rearrange("(p t) o -> p (t o)", t=PACK))
         xw = sb("xw", [P, S], U32)
 
         def queries(h):
             nc.vector.tensor_copy(xw[:, h * GW : (h + 1) * GW], xw_win[:].bitcast(U32).indirect(offs_sb[:, h * GW // 16 : (h + 1) * GW // 16]))
 
-        ww = sb("ww", [P, S], U32)
+        ww = reuse.tile([P, S], U32, name="ww", offset=8 * TABLE, align_bytes=64)
         y_scales = sb("y_scales", [P, S], U8)
         out_rows = out_0.rearrange("(p t) j -> p t j", t=PACK)
         out_words = words_of(out_1)
-        s_mid = sb("s_mid", [P, PACK, 2 * CH], F32)
+        shared = sb("shared", [P, 10 * CH], F32)
+        s_pair = [shared[:].rearrange("p (e w) -> p e w", e=2)[:, :, : 2 * CH], sb("s_pair1", [P, 2, 2 * CH], F32)[:]]
         s_last = ring.tile([P, PACK, CH], F32, name="s_last", offset=7 * TABLE, align_bytes=64)
-        s_sb = {1: s_mid, 3: s_last}
         u_sb = {}
-        s_side = sb("s_side", [P, CH], F32)
         yw = ring.tile([P, S], I32, name="yw", offset=5 * TABLE, align_bytes=64)
         zq = {}
         y_bank = {}
@@ -144,21 +139,26 @@ def tile_picked_temper_tanh_po_kernel(
                 stop=True,
             )
 
-        def scores_first():
-            side = psum.tile([P, CH], F32, name="y_bank3")
-            score(side[:], 3, 0, CH)
-            nc.scalar.copy(s_side[:], side[:])
-            bank = psum.tile([P, 3, CH], F32, name="s_bank0")
-            for t in range(3):
-                score(bank[:, t, :], t, 0, CH)
-            y_bank["s0"] = bank
+        s_first = {}
 
-        def scores_mid():
-            for pair in range(2):
-                bank = psum.tile([P, 2, 2 * CH], F32, name=f"s_bank{1 + pair}")
-                for e in range(2):
-                    score(bank[:, e, :], 2 * pair + e, CH, 3 * CH)
-                nc.scalar.copy(s_mid[:, 2 * pair : 2 * pair + 2, :], bank[:])
+        def scores_first():
+            for tag, ts in (("y_bank3", (0,)), ("y_bank0", (1,)), ("s_bank0", (2, 3))):
+                bank = psum.tile([P, len(ts), CH], F32, name=tag)
+                for e, t in enumerate(ts):
+                    score(bank[:, e, :], t, 0, CH)
+                if len(ts) == 2:
+                    held = ring.tile([P, len(ts), CH], F32, name="s_first2", offset=TABLE, align_bytes=64)
+                else:
+                    held = sb(f"s_first{ts[0]}", [P, len(ts), CH], F32)
+                nc.scalar.copy(held[:], bank[:])
+                for e, t in enumerate(ts):
+                    s_first[t] = held[:, e, :]
+
+        def scores_mid(pair):
+            bank = psum.tile([P, 2, 2 * CH], F32, name=f"s_bank{1 + pair}")
+            for e in range(2):
+                score(bank[:, e, :], 2 * pair + e, CH, 3 * CH)
+            nc.scalar.copy(s_pair[pair], bank[:])
 
         def scores_last():
             bank = psum.tile([P, PACK, CH], F32, name="s_bank3")
@@ -168,11 +168,8 @@ def tile_picked_temper_tanh_po_kernel(
 
         def temper_first():
             u = ring.tile([P, PACK, CH], F32, name="u_first", offset=0, align_bytes=64)
-            tg = ring.tile([P, 3, CH], F32, name="tg", offset=TABLE, align_bytes=64)
-            for t in range(3):
-                nc.vector.tensor_copy(tg[:, t, :], temp_sb[t][:].indirect(task_sb[:, : CH // 16]))
-            nc.vector.tensor_tensor(u[:, 3, :], temp_sb[3][:].indirect(task_sb[:, : CH // 16]), s_side[:], MULT)
-            nc.vector.tensor_tensor(u[:, :3, :], y_bank["s0"][:], tg[:], MULT)
+            for t in range(PACK):
+                nc.vector.tensor_tensor(u[:, t, :], temp_sb[t][:].indirect(task_sb[:, : CH // 16]), s_first[t], MULT)
             u_sb[0] = u[:]
 
         def temper(first, count):
@@ -180,20 +177,28 @@ def tile_picked_temper_tanh_po_kernel(
             u = ring.tile([P, PACK, width], F32, name=f"u{first}", offset=first * TABLE, align_bytes=64)
             for t in range(PACK):
                 nc.vector.tensor_tensor(
-                    u[:, t, :], temp_sb[t][:].indirect(task_sb[:, lo // 16 : (lo + width) // 16]), s_sb[first][:, t, :], MULT
+                    u[:, t, :], temp_sb[t][:].indirect(task_sb[:, lo // 16 : (lo + width) // 16]), s_pair[t // 2][:, t % 2, :], MULT
                 )
             for i in range(count):
                 u_sb[first + i] = u[:, :, i * CH : (i + 1) * CH]
 
+        u_last = shared[:, CH : 5 * CH]
+        u_sb[3] = u_last.rearrange("p (t j) -> p t j", t=PACK)
+
+        def temper_last(t):
+            nc.vector.tensor_tensor(
+                u_last[:, t * CH : (t + 1) * CH], temp_sb[t][:].indirect(task_sb[:, 3 * CH // 16 :]), s_last[:, t, :], MULT
+            )
+
         def hidden_first():
-            th = sb("th0", [P, PACK, CH], F32)
-            nc.scalar.activation(th[:, 3, :], u_sb[0][:, 3, :], ACT.Tanh, scale=0.0625)
+            th = ring.tile([P, PACK, CH], F32, name="th0", offset=4 * TABLE, align_bytes=64)
             nc.scalar.activation(th[:, :3, :], u_sb[0][:, :3, :], ACT.Tanh, scale=0.0625)
-            zp = ring.tile([P, PACK, CH], BF16, name="zp0", offset=4 * TABLE, align_bytes=64)
-            for t in (3, 0, 1, 2):
-                nc.scalar.activation(zp[:, t, :], th[:, t, :], ACT.Copy, scale=gn_sb[:, t : t + 1])
+            nc.scalar.activation(th[:, 3, :], u_sb[0][:, 3, :], ACT.Tanh, scale=0.0625)
+            zp = u_last[:, 3 * CH // 2 : 7 * CH // 2].bitcast(BF16)
+            for t in range(PACK):
+                nc.scalar.activation(zp[:, t * CH : (t + 1) * CH], th[:, t, :], ACT.Copy, scale=gn_sb[:, t : t + 1])
             zb = sb("zb0", [P, CH, PACK], BF16)
-            nc.scalar.copy(zb[:].rearrange("p (c i) t -> p c t i", i=4), zp[:].rearrange("p t (c i) -> p c t i", i=4))
+            nc.scalar.copy(zb[:].rearrange("p (c i) t -> p c t i", i=4), zp.rearrange("p (t c i) -> p c t i", t=PACK, i=4))
             zq[0] = zb
 
         th_sb = {}
@@ -215,6 +220,7 @@ def tile_picked_temper_tanh_po_kernel(
             zq[c] = zb
 
         y_sb = {}
+        z_first = []
 
         def values(c):
             if c in (1, 2):
@@ -223,6 +229,8 @@ def tile_picked_temper_tanh_po_kernel(
                 zw = sb(f"zw{c}", [P, CH], U32)
             zs = sb(f"zs{c}", [P, CH], U8)
             nc.vector.quantize_mx(out=zw[:].bitcast(FP8X4), scales=zs[:], in_=zq[c][:].rearrange("p j t -> p (j t)"))
+            if c == 0:
+                z_first.extend([zw, zs])
             groups = [(0, 2, "y_bank3"), (2, 4, "s_bank0")] if c == 3 else [(0, 4, f"y_bank{c}")]
             banks = []
             for lo, hi, tag in groups:
@@ -239,6 +247,19 @@ def tile_picked_temper_tanh_po_kernel(
                     )
                 banks.append((lo, hi, bank))
             y_bank[c] = banks
+
+        def warm_passes():
+            for tag in ("s_bank1", "s_bank2"):
+                bank = psum.tile([P, S], F32, name=tag)
+                nc.tensor.matmul_mx(
+                    out=bank[:],
+                    lhsT=z_first[0][:].bitcast(FP8X4),
+                    lhsT_scale=z_first[1][:],
+                    rhs=xw[:].bitcast(FP8X4),
+                    rhs_scale=xsc,
+                    start=True,
+                    stop=True,
+                )
 
         def result(c):
             y = sb(f"y{c}", [P, PACK, CH], F32)
@@ -270,19 +291,24 @@ def tile_picked_temper_tanh_po_kernel(
         queries(0)
         scores_first()
         queries(1)
-        scores_mid()
+        deal(ww[:].bitcast(I32), ww_raw[:])
+        scores_mid(0)
+        scores_mid(1)
         scores_last()
         temper_first()
-        deal(ww[:].bitcast(I32), ww_raw[:])
         temper(1, 2)
         hidden_first()
         nc.scalar.copy(s_last[:], y_bank["s3"][:])
-        temper(3, 1)
+        temper_last(0)
         values(0)
+        warm_passes()
+        temper_last(1)
+        temper_last(2)
+        temper_last(3)
         squash(1)
         squash(2)
-        squash(3)
         result(0)
+        squash(3)
         rounded(0)
         gain(1)
         gain(2)
@@ -293,9 +319,11 @@ def tile_picked_temper_tanh_po_kernel(
         planes(0)
         for c in range(1, S // CH):
             result(c)
-        for c in range(1, S // CH):
+        rounded(1)
+        for c in range(2, S // CH):
             rounded(c)
-            planes(c)
+            planes(c - 1)
+        planes(3)
         for q in range(4):
             eng = nc.scalar if q % 2 else nc.sync
             eng.dma_start(out_2[0, 4 * q : 4 * q + 4, :].bitcast(I32), y_scales[32 * q : 32 * q + 4, :].bitcast(I32))

@@ -44,11 +44,9 @@ def tile_picked_temper_tanh_po_kernel(
         dsc_win = sb("dsc_win", [P, TABLE], U8)
         xsc_win = sb("xsc_win", [P, TABLE], U8)
         wsc_raw = sb("wsc_raw", [P, S], U8)
-        warm = sb("warm", [P, 1], F32)
         dw_win = reuse.tile([P, TABLE], I32, name="dw_win", offset=4 * TABLE)
         xw_win = reuse.tile([P, TABLE], I32, name="xw_win", offset=8 * TABLE, align_bytes=64)
         ww_raw = sb("ww_raw", [P, S], I32)
-        warm_out = sb("warm_out", [P, 1], F32)
 
 
         for win in (wsc_raw, dsc_win, xsc_win):
@@ -64,8 +62,6 @@ def tile_picked_temper_tanh_po_kernel(
         nc.sync.dma_start(ww_raw[:], words_of(w1_words))
         temp_rows = temp.rearrange("(p t) u -> p t u", t=PACK)
         temp_sb = []
-        nc.vector.memset(warm[:], 0.0)
-        nc.scalar.activation(warm_out[:], warm[:], ACT.Tanh)
 
         def deal_bytes(dst, src):
             nc.vector.tensor_copy(dst.rearrange("p (t m) -> p t m", t=PACK), src.rearrange("p (m t) -> p t m", t=PACK))
@@ -220,7 +216,6 @@ def tile_picked_temper_tanh_po_kernel(
             zq[c] = zb
 
         y_sb = {}
-        z_first = []
 
         def values(c):
             if c in (1, 2):
@@ -229,8 +224,6 @@ def tile_picked_temper_tanh_po_kernel(
                 zw = sb(f"zw{c}", [P, CH], U32)
             zs = sb(f"zs{c}", [P, CH], U8)
             nc.vector.quantize_mx(out=zw[:].bitcast(FP8X4), scales=zs[:], in_=zq[c][:].rearrange("p j t -> p (j t)"))
-            if c == 0:
-                z_first.extend([zw, zs])
             groups = [(0, 2, "y_bank3"), (2, 4, "s_bank0")] if c == 3 else [(0, 4, f"y_bank{c}")]
             banks = []
             for lo, hi, tag in groups:
@@ -247,19 +240,6 @@ def tile_picked_temper_tanh_po_kernel(
                     )
                 banks.append((lo, hi, bank))
             y_bank[c] = banks
-
-        def warm_passes():
-            for tag in ("s_bank1", "s_bank2"):
-                bank = psum.tile([P, S], F32, name=tag)
-                nc.tensor.matmul_mx(
-                    out=bank[:],
-                    lhsT=z_first[0][:].bitcast(FP8X4),
-                    lhsT_scale=z_first[1][:],
-                    rhs=xw[:].bitcast(FP8X4),
-                    rhs_scale=xsc,
-                    start=True,
-                    stop=True,
-                )
 
         def result(c):
             y = sb(f"y{c}", [P, PACK, CH], F32)
@@ -301,7 +281,6 @@ def tile_picked_temper_tanh_po_kernel(
         nc.scalar.copy(s_last[:], y_bank["s3"][:])
         temper_last(0)
         values(0)
-        warm_passes()
         temper_last(1)
         temper_last(2)
         temper_last(3)

@@ -43,37 +43,31 @@ def tile_picked_temper_tanh_po_kernel(
         task_sb = sb("task_sb", [P, S // 16], U16)
         dsc_win = sb("dsc_win", [P, TABLE], U8)
         xsc_win = sb("xsc_win", [P, TABLE], U8)
-        wsc_raw = sb("wsc_raw", [P, S], U8)
+        wsc_raw = ring.tile([P, S], U8, name="wsc_raw", offset=3 * TABLE, align_bytes=64)
         dw_win = reuse.tile([P, TABLE], I32, name="dw_win", offset=4 * TABLE)
         xw_win = reuse.tile([P, TABLE], I32, name="xw_win", offset=8 * TABLE, align_bytes=64)
-        ww_raw = sb("ww_raw", [P, S], I32)
 
 
-        for win in (wsc_raw, dsc_win, xsc_win):
+        for win in (dsc_win, xsc_win, wsc_raw):
             nc.vector.memset(win[:].bitcast(I32), 0)
         nc.sync.dma_start(kidx_sb[:], kidx)
-        nc.scalar.dma_start(wsc_raw[0:P:8, :].bitcast(I32), w1_scales[0].bitcast(I32))
         nc.sync.dma_start(offs_sb[:], offs)
         nc.sync.dma_start(dsc_win[0:P:8, :].bitcast(I32), d_scales[0].bitcast(I32))
         nc.sync.dma_start(task_sb[:], task)
         nc.sync.dma_start(xsc_win[0:P:8, :].bitcast(I32), x_scales[0].bitcast(I32))
         nc.sync.dma_start(dw_win[:], words_of(d_words))
         nc.sync.dma_start(xw_win[:], words_of(x_words))
-        nc.sync.dma_start(ww_raw[:], words_of(w1_words))
+        nc.sync.dma_start(wsc_raw[0:P:8, :].bitcast(I32), w1_scales[0].bitcast(I32))
         temp_rows = temp.rearrange("(p t) u -> p t u", t=PACK)
-        temp_sb = []
+        temp_sb = [sb("temp0", [P, S], F32)]
+        nc.sync.dma_start(temp_sb[0][:], temp_rows[:, 0, :])
 
         def deal_bytes(dst, src):
             nc.vector.tensor_copy(dst.rearrange("p (t m) -> p t m", t=PACK), src.rearrange("p (m t) -> p t m", t=PACK))
 
-        def deal(dst, src):
-            nc.vector.tensor_copy(
-                dst.rearrange("p (t c i) -> p c t i", t=PACK, i=4), src.rearrange("p (c i t) -> p c t i", t=PACK, i=4)
-            )
 
-        planes3 = sb("planes3", [P, 3 * S], U8)
-        dsc, wsc, xsc = planes3[:, :S], planes3[:, S : 2 * S], planes3[:, 2 * S :]
-        deal_bytes(wsc, wsc_raw[:])
+        planes3 = sb("planes2", [P, 2 * S], U8)
+        dsc, xsc = planes3[:, :S], planes3[:, S:]
         dsc_g = sb("dsc_g", [P, S], U8)
         for h in range(2):
             nc.vector.tensor_copy(dsc_g[:, h * GW : (h + 1) * GW], dsc_win[:].indirect(kidx_sb[:, h * GW // 16 : (h + 1) * GW // 16]))
@@ -101,10 +95,12 @@ def tile_picked_temper_tanh_po_kernel(
                 dw[:].bitcast(I32).rearrange("p (t h c i) -> p h c t i", t=PACK, h=2, i=4)[:, h],
                 dw_g[:].bitcast(I32).rearrange("p (h c i t) -> p h c t i", t=PACK, h=2, i=4)[:, h],
             )
-        for t in range(PACK):
-            late = reuse.tile([P, S], F32, name=f"temp{t}", offset=t * TABLE)
+        for t in range(1, PACK):
+            late = reuse.tile([P, S], F32, name=f"temp{t}", offset=(t - 1) * TABLE)
             nc.sync.dma_start(late[:], temp_rows[:, t, :])
             temp_sb.append(late)
+        ww_raw = reuse.tile([P, S], I32, name="ww_raw", offset=4 * TABLE)
+        nc.sync.dma_start(ww_raw[:], words_of(w1_words))
         gn_sb = reuse.tile([P, PACK], F32, name="gn_sb", offset=5 * TABLE)
         nc.sync.dma_start(gn_sb[:], gn.rearrange("(p t) o -> p (t o)", t=PACK))
         xw = sb("xw", [P, S], U32)
@@ -112,17 +108,16 @@ def tile_picked_temper_tanh_po_kernel(
         def queries(h):
             nc.vector.tensor_copy(xw[:, h * GW : (h + 1) * GW], xw_win[:].bitcast(U32).indirect(offs_sb[:, h * GW // 16 : (h + 1) * GW // 16]))
 
-        ww = reuse.tile([P, S], U32, name="ww", offset=8 * TABLE, align_bytes=64)
+        ww = sb("ww", [P, S], U32)
+        wsc_t = reuse.tile([P, S], U8, name="wsc", offset=9 * TABLE, align_bytes=64)
+        wsc = wsc_t[:]
         y_scales = sb("y_scales", [P, S], U8)
+        yw = sb("yw", [P, S], I32)
         out_rows = out_0.rearrange("(p t) j -> p t j", t=PACK)
         out_words = words_of(out_1)
-        shared = sb("shared", [P, 10 * CH], F32)
-        s_pair = [shared[:].rearrange("p (e w) -> p e w", e=2)[:, :, : 2 * CH], sb("s_pair1", [P, 2, 2 * CH], F32)[:]]
-        s_last = ring.tile([P, PACK, CH], F32, name="s_last", offset=7 * TABLE, align_bytes=64)
-        u_sb = {}
-        yw = ring.tile([P, S], I32, name="yw", offset=5 * TABLE, align_bytes=64)
-        zq = {}
-        y_bank = {}
+
+        def tasks(lo, hi):
+            return task_sb[:, lo // 16 : hi // 16]
 
         def score(out, t, lo, hi):
             nc.tensor.matmul_mx(
@@ -135,97 +130,38 @@ def tile_picked_temper_tanh_po_kernel(
                 stop=True,
             )
 
-        s_first = {}
+        def scores(tag, ts, lo, hi):
+            bank = psum.tile([P, len(ts), hi - lo], F32, name=tag)
+            for e, t in enumerate(ts):
+                score(bank[:, e, :], t, lo, hi)
+            return bank
 
-        def scores_first():
-            for tag, ts in (("y_bank3", (0,)), ("y_bank0", (1,)), ("s_bank0", (2, 3))):
-                bank = psum.tile([P, len(ts), CH], F32, name=tag)
-                for e, t in enumerate(ts):
-                    score(bank[:, e, :], t, 0, CH)
-                if len(ts) == 2:
-                    held = ring.tile([P, len(ts), CH], F32, name="s_first2", offset=TABLE, align_bytes=64)
-                else:
-                    held = sb(f"s_first{ts[0]}", [P, len(ts), CH], F32)
-                nc.scalar.copy(held[:], bank[:])
-                for e, t in enumerate(ts):
-                    s_first[t] = held[:, e, :]
+        def look_up(out, t, lo, hi):
+            nc.scalar.activation(out, temp_sb[t][:].indirect(tasks(lo, hi)), ACT.Copy)
 
-        def scores_mid(pair):
-            bank = psum.tile([P, 2, 2 * CH], F32, name=f"s_bank{1 + pair}")
-            for e in range(2):
-                score(bank[:, e, :], 2 * pair + e, CH, 3 * CH)
-            nc.scalar.copy(s_pair[pair], bank[:])
+        def fused(out, t, lo, hi, held):
+            nc.vector.tensor_tensor(out, temp_sb[t][:].indirect(tasks(lo, hi)), held, MULT)
 
-        def scores_last():
-            bank = psum.tile([P, PACK, CH], F32, name="s_bank3")
-            for t in range(PACK):
-                score(bank[:, t, :], t, 3 * CH, S)
-            y_bank["s3"] = bank
-
-        def temper_first():
-            u = ring.tile([P, PACK, CH], F32, name="u_first", offset=0, align_bytes=64)
-            for t in range(PACK):
-                nc.vector.tensor_tensor(u[:, t, :], temp_sb[t][:].indirect(task_sb[:, : CH // 16]), s_first[t], MULT)
-            u_sb[0] = u[:]
-
-        def temper(first, count):
-            lo, width = first * CH, count * CH
-            u = ring.tile([P, PACK, width], F32, name=f"u{first}", offset=first * TABLE, align_bytes=64)
-            for t in range(PACK):
-                nc.vector.tensor_tensor(
-                    u[:, t, :], temp_sb[t][:].indirect(task_sb[:, lo // 16 : (lo + width) // 16]), s_pair[t // 2][:, t % 2, :], MULT
-                )
-            for i in range(count):
-                u_sb[first + i] = u[:, :, i * CH : (i + 1) * CH]
-
-        u_last = shared[:, CH : 5 * CH]
-        u_sb[3] = u_last.rearrange("p (t j) -> p t j", t=PACK)
-
-        def temper_last(t):
-            nc.vector.tensor_tensor(
-                u_last[:, t * CH : (t + 1) * CH], temp_sb[t][:].indirect(task_sb[:, 3 * CH // 16 :]), s_last[:, t, :], MULT
-            )
-
-        def hidden_first():
-            th = ring.tile([P, PACK, CH], F32, name="th0", offset=4 * TABLE, align_bytes=64)
-            nc.scalar.activation(th[:, :3, :], u_sb[0][:, :3, :], ACT.Tanh, scale=0.0625)
-            nc.scalar.activation(th[:, 3, :], u_sb[0][:, 3, :], ACT.Tanh, scale=0.0625)
-            zp = u_last[:, 3 * CH // 2 : 7 * CH // 2].bitcast(BF16)
-            for t in range(PACK):
-                nc.scalar.activation(zp[:, t * CH : (t + 1) * CH], th[:, t, :], ACT.Copy, scale=gn_sb[:, t : t + 1])
-            zb = sb("zb0", [P, CH, PACK], BF16)
-            nc.scalar.copy(zb[:].rearrange("p (c i) t -> p c t i", i=4), zp.rearrange("p (t c i) -> p c t i", t=PACK, i=4))
-            zq[0] = zb
-
-        th_sb = {}
-        th_mid = ring.tile([P, 3 * CH, PACK], F32, name="th_mid", offset=4 * TABLE, align_bytes=64)
+        u_sb, th_sb, zq, y_bank, y_sb, yb_sb = {}, {}, {}, {}, {}, {}
 
         def squash(c):
-            th = th_mid[:, (c - 1) * CH : c * CH, :]
+            th = sb(f"th{c}", [P, CH, PACK], F32)
             nc.scalar.activation(
-                th.rearrange("p (c i) t -> p c t i", i=4),
-                u_sb[c].rearrange("p t (c i) -> p c t i", i=4),
-                ACT.Tanh,
-                scale=0.0625,
+                th[:].rearrange("p (c i) t -> p c t i", i=4), u_sb[c].rearrange("p t (c i) -> p c t i", i=4), ACT.Tanh, scale=0.0625
             )
             th_sb[c] = th
 
         def gain(c):
             zb = sb(f"zb{c}", [P, CH, PACK], BF16)
-            nc.vector.tensor_tensor(zb[:], th_sb[c], gn_sb[:].unsqueeze(1).to_broadcast([P, CH, PACK]), MULT)
+            nc.vector.tensor_tensor(zb[:], th_sb[c][:], gn_sb[:].unsqueeze(1).to_broadcast([P, CH, PACK]), MULT)
             zq[c] = zb
 
-        y_sb = {}
-
         def values(c):
-            if c in (1, 2):
-                zw = ring.tile([P, CH], U32, name=f"zw{c}", offset=(c + 1) * TABLE, align_bytes=64)
-            else:
-                zw = sb(f"zw{c}", [P, CH], U32)
+            zw = sb(f"zw{c}", [P, CH], U32)
             zs = sb(f"zs{c}", [P, CH], U8)
             nc.vector.quantize_mx(out=zw[:].bitcast(FP8X4), scales=zs[:], in_=zq[c][:].rearrange("p j t -> p (j t)"))
-            groups = [(0, 2, "y_bank3"), (2, 4, "s_bank0")] if c == 3 else [(0, 4, f"y_bank{c}")]
-            banks = []
+            groups = [(0, 2, "bank2"), (2, 4, "bank3")] if c == 3 else [(0, 4, ("bank7", "bank0", "bank1")[c])]
+            y_bank[c] = []
             for lo, hi, tag in groups:
                 bank = psum.tile([P, hi - lo, CH], F32, name=tag)
                 for t in range(lo, hi):
@@ -238,8 +174,7 @@ def tile_picked_temper_tanh_po_kernel(
                         start=True,
                         stop=True,
                     )
-                banks.append((lo, hi, bank))
-            y_bank[c] = banks
+                y_bank[c].append((lo, hi, bank))
 
         def result(c):
             y = sb(f"y{c}", [P, PACK, CH], F32)
@@ -248,60 +183,88 @@ def tile_picked_temper_tanh_po_kernel(
             nc.sync.dma_start(out_rows[:, :, c * CH : (c + 1) * CH], y[:])
             y_sb[c] = y
 
-        yb_sb = {}
-
         def rounded(c):
             yb = sb(f"yb{c}", [P, CH, PACK], BF16)
             if c == 0:
                 nc.scalar.copy(yb[:], y_bank[c][0][2][:].rearrange("p t j -> p j t"))
             else:
-                nc.vector.tensor_copy(
-                    yb[:].rearrange("p (c i) t -> p c t i", i=4), y_sb[c][:].rearrange("p t (c i) -> p c t i", i=4)
-                )
+                nc.vector.tensor_copy(yb[:].rearrange("p (c i) t -> p c t i", i=4), y_sb[c][:].rearrange("p t (c i) -> p c t i", i=4))
             yb_sb[c] = yb
 
         def planes(c):
             nc.vector.quantize_mx(
-                out=yw[:, c * CH : (c + 1) * CH].bitcast(FP8X4), scales=y_scales[:, c * CH : (c + 1) * CH], in_=yb_sb[c][:].rearrange("p j t -> p (j t)")
+                out=yw[:, c * CH : (c + 1) * CH].bitcast(FP8X4),
+                scales=y_scales[:, c * CH : (c + 1) * CH],
+                in_=yb_sb[c][:].rearrange("p j t -> p (j t)"),
             )
-            if c != 1:
-                lo = CH if c == 2 else c * CH
+            if c >= 2:
+                lo = 0 if c == 2 else c * CH
                 nc.sync.dma_start(out_words[:, lo : (c + 1) * CH], yw[:, lo : (c + 1) * CH])
 
+        tg_first = sb("tg_first", [P, CH], F32)
+        look_up(tg_first[:], 0, 0, CH)
         queries(0)
-        scores_first()
+        first0 = scores("bank0", (0,), 0, CH)
+        s_first1 = ring.tile([P, 1, CH], F32, name="s_first1", offset=5 * TABLE, align_bytes=64)
+        nc.scalar.copy(s_first1[:], scores("bank1", (1,), 0, CH)[:])
+        s_first23 = ring.tile([P, 2, CH], F32, name="s_first23", offset=0, align_bytes=64)
+        nc.scalar.copy(s_first23[:], scores("bank2", (2, 3), 0, CH)[:])
         queries(1)
-        deal(ww[:].bitcast(I32), ww_raw[:])
-        scores_mid(0)
-        scores_mid(1)
-        scores_last()
-        temper_first()
-        temper(1, 2)
-        hidden_first()
-        nc.scalar.copy(s_last[:], y_bank["s3"][:])
-        temper_last(0)
+        deal_bytes(wsc, wsc_raw[:])
+        for r in range(1, 4):
+            nc.sync.dma_start(wsc_t[r:P:32, :].bitcast(I32), wsc_t[8 * r : P : 32, :].bitcast(I32))
+        tg_mid = ring.tile([P, 2 * CH], F32, name="tg_mid", offset=3 * TABLE, align_bytes=64)
+        look_up(tg_mid[:], 0, CH, 3 * CH)
+        mid0 = scores("bank3", (0,), CH, 3 * CH)
+        s_mid1 = sb("s_mid1", [P, 1, 2 * CH], F32)
+        nc.scalar.copy(s_mid1[:], scores("bank4", (1,), CH, 3 * CH)[:])
+        s_mid23 = sb("s_mid23", [P, 2, 2 * CH], F32)
+        nc.scalar.copy(s_mid23[:], scores("bank5", (2, 3), CH, 3 * CH)[:])
+        last = scores("bank6", range(PACK), 3 * CH, S)
+
+        u_first = sb("u_first", [P, PACK, CH], F32)
+        nc.vector.tensor_tensor(u_first[:, 0, :], first0[:, 0, :], tg_first[:], MULT)
+        fused(u_first[:, 1, :], 1, 0, CH, s_first1[:, 0, :])
+        for t in (2, 3):
+            fused(u_first[:, t, :], t, 0, CH, s_first23[:, t - 2, :])
+        u_sb[0] = u_first[:]
+        squash(0)
+
+        u_mid = ring.tile([P, PACK, 2 * CH], F32, name="u_mid", offset=0, align_bytes=64)
+        nc.vector.tensor_tensor(u_mid[:, 0, :], mid0[:, 0, :], tg_mid[:], MULT)
+        fused(u_mid[:, 1, :], 1, CH, 3 * CH, s_mid1[:, 0, :])
+        for t in (2, 3):
+            fused(u_mid[:, t, :], t, CH, 3 * CH, s_mid23[:, t - 2, :])
+        u_sb[1], u_sb[2] = u_mid[:, :, :CH], u_mid[:, :, CH:]
+
+        tg_last = ring.tile([P, PACK, CH], F32, name="tg_last", offset=5 * TABLE, align_bytes=64)
+        for t in range(PACK):
+            look_up(tg_last[:, t, :], t, 3 * CH, S)
+        nc.scalar.copy(
+            ww[:].rearrange("p (t c i) -> p c t i", t=PACK, i=4), ww_raw[:].bitcast(U32).rearrange("p (c i t) -> p c t i", t=PACK, i=4)
+        )
+        gain(0)
+        u_last = sb("u_last", [P, PACK, CH], F32)
+        nc.vector.tensor_tensor(u_last[:], last[:], tg_last[:], MULT)
+        u_sb[3] = u_last[:]
+        for c in range(1, 4):
+            squash(c)
         values(0)
-        temper_last(1)
-        temper_last(2)
-        temper_last(3)
-        squash(1)
-        squash(2)
-        result(0)
-        squash(3)
-        rounded(0)
         gain(1)
         gain(2)
         values(1)
         gain(3)
         values(2)
         values(3)
-        planes(0)
-        for c in range(1, S // CH):
+        result(0)
+        rounded(0)
+        for c in range(1, 4):
             result(c)
-        rounded(1)
-        for c in range(2, S // CH):
+        for c in range(1, 3):
             rounded(c)
             planes(c - 1)
+        planes(2)
+        rounded(3)
         planes(3)
         for q in range(4):
             eng = nc.scalar if q % 2 else nc.sync

@@ -16,13 +16,19 @@ P = 128
 PACK = 4
 TABLE = 2048
 S = 512
-CH = 128
-GW = 256
+CHUNK = 128
+HALF = S // 2
+LINE = 4
+SLOT = 2048
 FLOPS = 2 * 2 * 512 * 512 * 512
 
 
 def words_of(dram):
     return dram[0].rearrange("p n t -> p (n t)").bitcast(I32)
+
+
+def entries(list_sb, lo, hi):
+    return list_sb[:, lo // 16 : hi // 16]
 
 
 def tile_picked_temper_tanh_po_kernel(
@@ -31,241 +37,238 @@ def tile_picked_temper_tanh_po_kernel(
     nc = tc.nc
     with ExitStack() as ctx:
         keep = ctx.enter_context(tc.tile_pool(name="keep", bufs=1))
-        ring = ctx.enter_context(tc.tile_pool(name="ring", bufs=1))
-        reuse = ctx.enter_context(tc.tile_pool(name="reuse", bufs=1))
+        work = ctx.enter_context(tc.tile_pool(name="work", bufs=1))
+        loads = ctx.enter_context(tc.tile_pool(name="loads", bufs=1))
         psum = ctx.enter_context(tc.psum_pool(name="psum", bufs=1))
 
         def sb(name, shape, dtype):
             return keep.tile(shape, dtype, name=name, align_bytes=64)
 
+        def move_scale_rows(tile, queues):
+            for r, queue in zip(range(1, PACK), queues):
+                queue.dma_start(tile[r:P:32, :].bitcast(I32), tile[8 * r : P : 32, :].bitcast(I32))
+
         kidx_sb = sb("kidx_sb", [P, S // 16], U16)
         offs_sb = sb("offs_sb", [P, S // 16], U16)
         task_sb = sb("task_sb", [P, S // 16], U16)
-        dsc_win = sb("dsc_win", [P, TABLE], U8)
-        xsc_win = sb("xsc_win", [P, TABLE], U8)
-        wsc_raw = ring.tile([P, S], U8, name="wsc_raw", offset=3 * TABLE, align_bytes=64)
-        dw_win = reuse.tile([P, TABLE], I32, name="dw_win", offset=4 * TABLE)
-        xw_win = reuse.tile([P, TABLE], I32, name="xw_win", offset=8 * TABLE, align_bytes=64)
-
-
-        for win in (dsc_win, xsc_win, wsc_raw):
-            nc.vector.memset(win[:].bitcast(I32), 0)
+        d_scale_table = sb("d_scale_table", [P, TABLE], U8)
+        x_scale_table = sb("x_scale_table", [P, TABLE], U8)
+        w_scale_rows = work.tile([P, S], U8, name="w_scale_rows", offset=3 * SLOT, align_bytes=64)
+        d_word_table = loads.tile([P, TABLE], I32, name="d_word_table", offset=4 * SLOT)
+        x_word_table = loads.tile([P, TABLE], I32, name="x_word_table", offset=8 * SLOT, align_bytes=64)
+        for rows in (d_scale_table, x_scale_table, w_scale_rows):
+            nc.vector.memset(rows[:].bitcast(I32), 0)
         nc.sync.dma_start(kidx_sb[:], kidx)
         nc.sync.dma_start(offs_sb[:], offs)
-        nc.sync.dma_start(dsc_win[0:P:8, :].bitcast(I32), d_scales[0].bitcast(I32))
+        nc.sync.dma_start(d_scale_table[0:P:8, :].bitcast(I32), d_scales[0].bitcast(I32))
         nc.sync.dma_start(task_sb[:], task)
-        nc.sync.dma_start(xsc_win[0:P:8, :].bitcast(I32), x_scales[0].bitcast(I32))
-        nc.sync.dma_start(dw_win[:], words_of(d_words))
-        nc.sync.dma_start(xw_win[:], words_of(x_words))
-        nc.sync.dma_start(wsc_raw[0:P:8, :].bitcast(I32), w1_scales[0].bitcast(I32))
-        temp_rows = temp.rearrange("(p t) u -> p t u", t=PACK)
+        nc.sync.dma_start(x_scale_table[0:P:8, :].bitcast(I32), x_scales[0].bitcast(I32))
+        nc.sync.dma_start(d_word_table[:], words_of(d_words))
+        nc.sync.dma_start(x_word_table[:], words_of(x_words))
+        nc.sync.dma_start(w_scale_rows[0:P:8, :].bitcast(I32), w1_scales[0].bitcast(I32))
+        temp_planes = temp.rearrange("(p t) u -> p t u", t=PACK)
         temp_sb = [sb("temp0", [P, S], F32)]
-        nc.sync.dma_start(temp_sb[0][:], temp_rows[:, 0, :])
+        nc.sync.dma_start(temp_sb[0][:], temp_planes[:, 0, :])
 
-        def deal_bytes(dst, src):
-            nc.vector.tensor_copy(dst.rearrange("p (t m) -> p t m", t=PACK), src.rearrange("p (m t) -> p t m", t=PACK))
-
-
-        planes3 = sb("planes2", [P, 2 * S], U8)
-        dsc, xsc = planes3[:, :S], planes3[:, S:]
-        dsc_g = sb("dsc_g", [P, S], U8)
+        score_scales = sb("score_scales", [P, 2 * S], U8)
+        key_scales, query_scales = score_scales[:, :S], score_scales[:, S:]
+        d_scales_picked = sb("d_scales_picked", [P, S], U8)
         for h in range(2):
-            nc.vector.tensor_copy(dsc_g[:, h * GW : (h + 1) * GW], dsc_win[:].indirect(kidx_sb[:, h * GW // 16 : (h + 1) * GW // 16]))
-
-        def deal_half(h):
             nc.vector.tensor_copy(
-                dsc.rearrange("p (t h m) -> p h t m", t=PACK, h=2)[:, h], dsc_g[:].rearrange("p (h m t) -> p h t m", t=PACK, h=2)[:, h]
+                d_scales_picked[:, h * HALF : (h + 1) * HALF], d_scale_table[:].indirect(entries(kidx_sb, h * HALF, (h + 1) * HALF))
             )
-
-        xsc_g = reuse.tile([P, 2 * TABLE + S], U8, name="xsc_g", offset=TABLE - S // 2)[:, :S]
-        nc.vector.tensor_copy(xsc_g, xsc_win[:].indirect(offs_sb[:]))
-        deal_half(0)
-        deal_half(1)
-        nc.vector.tensor_copy(xsc.bitcast(I32), xsc_g.bitcast(I32))
-        for r in range(1, 4):
-            (nc.scalar if r == 2 else nc.sync).dma_start(planes3[r:P:32, :].bitcast(I32), planes3[8 * r : P : 32, :].bitcast(I32))
-        dw_g = sb("dw_g", [P, S], U32)
-        dw = sb("dw", [P, S], U32)
+        x_scales_picked = loads.tile([P, S], U8, name="x_scales_picked", offset=SLOT - S // 2)
+        nc.vector.tensor_copy(x_scales_picked[:], x_scale_table[:].indirect(offs_sb[:]))
         for h in range(2):
             nc.vector.tensor_copy(
-                dw_g[:, h * GW : (h + 1) * GW], dw_win[:].bitcast(U32).indirect(kidx_sb[:, h * GW // 16 : (h + 1) * GW // 16])
+                key_scales.rearrange("p (t h m) -> p h t m", t=PACK, h=2)[:, h],
+                d_scales_picked[:].rearrange("p (h m t) -> p h t m", t=PACK, h=2)[:, h],
+            )
+        nc.vector.tensor_copy(query_scales.bitcast(I32), x_scales_picked[:].bitcast(I32))
+        move_scale_rows(score_scales, (nc.sync, nc.scalar, nc.sync))
+
+        d_words_picked = sb("d_words_picked", [P, S], U32)
+        keys = sb("keys", [P, S], U32)
+        for h in range(2):
+            nc.vector.tensor_copy(
+                d_words_picked[:, h * HALF : (h + 1) * HALF],
+                d_word_table[:].bitcast(U32).indirect(entries(kidx_sb, h * HALF, (h + 1) * HALF)),
             )
         for h in range(2):
             nc.vector.tensor_copy(
-                dw[:].bitcast(I32).rearrange("p (t h c i) -> p h c t i", t=PACK, h=2, i=4)[:, h],
-                dw_g[:].bitcast(I32).rearrange("p (h c i t) -> p h c t i", t=PACK, h=2, i=4)[:, h],
+                keys[:].bitcast(I32).rearrange("p (t h c i) -> p h c t i", t=PACK, h=2, i=LINE)[:, h],
+                d_words_picked[:].bitcast(I32).rearrange("p (h c i t) -> p h c t i", t=PACK, h=2, i=LINE)[:, h],
             )
-        for t in range(1, PACK):
-            late = reuse.tile([P, S], F32, name=f"temp{t}", offset=(t - 1) * TABLE)
-            nc.sync.dma_start(late[:], temp_rows[:, t, :])
-            temp_sb.append(late)
-        ww_raw = reuse.tile([P, S], I32, name="ww_raw", offset=4 * TABLE)
-        nc.sync.dma_start(ww_raw[:], words_of(w1_words))
-        gn_sb = reuse.tile([P, PACK], F32, name="gn_sb", offset=5 * TABLE)
+
+        for t, slot in ((1, 0), (2, 1), (3, 6)):
+            plane = loads.tile([P, S], F32, name=f"temp{t}", offset=slot * SLOT)
+            nc.sync.dma_start(plane[:], temp_planes[:, t, :])
+            temp_sb.append(plane)
+        w_words = loads.tile([P, S], I32, name="w_words", offset=4 * SLOT)
+        nc.sync.dma_start(w_words[:], words_of(w1_words))
+        gn_sb = loads.tile([P, PACK], F32, name="gn_sb", offset=5 * SLOT)
         nc.sync.dma_start(gn_sb[:], gn.rearrange("(p t) o -> p (t o)", t=PACK))
-        xw = sb("xw", [P, S], U32)
 
-        def queries(h):
-            nc.vector.tensor_copy(xw[:, h * GW : (h + 1) * GW], xw_win[:].bitcast(U32).indirect(offs_sb[:, h * GW // 16 : (h + 1) * GW // 16]))
-
-        ww = sb("ww", [P, S], U32)
-        wsc_t = reuse.tile([P, S], U8, name="wsc", offset=9 * TABLE, align_bytes=64)
-        wsc = wsc_t[:]
+        queries = sb("queries", [P, S], U32)
+        values = sb("values", [P, S], U32)
+        value_scales = loads.tile([P, S], U8, name="value_scales", offset=9 * SLOT, align_bytes=64)
         y_scales = sb("y_scales", [P, S], U8)
-        yw = sb("yw", [P, S], I32)
-        out_rows = out_0.rearrange("(p t) j -> p t j", t=PACK)
+        y_words = sb("y_words", [P, S], I32)
+        out_planes = out_0.rearrange("(p t) j -> p t j", t=PACK)
         out_words = words_of(out_1)
 
-        def tasks(lo, hi):
-            return task_sb[:, lo // 16 : hi // 16]
+        def pick_queries(lo, hi):
+            nc.vector.tensor_copy(queries[:, lo:hi], x_word_table[:].bitcast(U32).indirect(entries(offs_sb, lo, hi)))
 
-        def score(out, t, lo, hi):
-            nc.tensor.matmul_mx(
-                out=out,
-                lhsT=dw[:, t * P : (t + 1) * P].bitcast(FP8X4),
-                lhsT_scale=dsc[:, t * P : (t + 1) * P],
-                rhs=xw[:, lo:hi].bitcast(FP8X4),
-                rhs_scale=xsc[:, lo:hi],
-                start=True,
-                stop=True,
-            )
-
-        def scores(tag, ts, lo, hi):
-            bank = psum.tile([P, len(ts), hi - lo], F32, name=tag)
-            for e, t in enumerate(ts):
-                score(bank[:, e, :], t, lo, hi)
+        def scores(bank_name, planes, lo, hi):
+            bank = psum.tile([P, len(planes), hi - lo], F32, name=bank_name)
+            for e, t in enumerate(planes):
+                nc.tensor.matmul_mx(
+                    out=bank[:, e, :],
+                    lhsT=keys[:, t * P : (t + 1) * P].bitcast(FP8X4),
+                    lhsT_scale=key_scales[:, t * P : (t + 1) * P],
+                    rhs=queries[:, lo:hi].bitcast(FP8X4),
+                    rhs_scale=query_scales[:, lo:hi],
+                    start=True,
+                    stop=True,
+                )
             return bank
 
         def look_up(out, t, lo, hi):
-            nc.scalar.activation(out, temp_sb[t][:].indirect(tasks(lo, hi)), ACT.Copy)
+            nc.scalar.activation(out, temp_sb[t][:].indirect(entries(task_sb, lo, hi)), ACT.Copy)
 
-        def fused(out, t, lo, hi, held):
-            nc.vector.tensor_tensor(out, temp_sb[t][:].indirect(tasks(lo, hi)), held, MULT)
+        def look_up_times(out, t, lo, hi, copied_scores):
+            nc.vector.tensor_tensor(out, temp_sb[t][:].indirect(entries(task_sb, lo, hi)), copied_scores, MULT)
 
-        u_sb, th_sb, zq, y_bank, y_sb, yb_sb = {}, {}, {}, {}, {}, {}
+        tempered, squashed, z_rounded, y_banks, y_sb, y_rounded = {}, {}, {}, {}, {}, {}
 
         def squash(c):
-            th = sb(f"th{c}", [P, CH, PACK], F32)
+            squashed[c] = sb(f"squashed{c}", [P, CHUNK, PACK], F32)
             nc.scalar.activation(
-                th[:].rearrange("p (c i) t -> p c t i", i=4), u_sb[c].rearrange("p t (c i) -> p c t i", i=4), ACT.Tanh, scale=0.0625
+                squashed[c][:].rearrange("p (c i) t -> p c t i", i=LINE),
+                tempered[c].rearrange("p t (c i) -> p c t i", i=LINE),
+                ACT.Tanh,
+                scale=0.0625,
             )
-            th_sb[c] = th
 
         def gain(c):
-            zb = sb(f"zb{c}", [P, CH, PACK], BF16)
-            nc.vector.tensor_tensor(zb[:], th_sb[c][:], gn_sb[:].unsqueeze(1).to_broadcast([P, CH, PACK]), MULT)
-            zq[c] = zb
+            z_rounded[c] = sb(f"z_rounded{c}", [P, CHUNK, PACK], BF16)
+            nc.vector.tensor_tensor(z_rounded[c][:], squashed[c][:], gn_sb[:].unsqueeze(1).to_broadcast([P, CHUNK, PACK]), MULT)
 
-        def values(c):
-            zw = sb(f"zw{c}", [P, CH], U32)
-            zs = sb(f"zs{c}", [P, CH], U8)
-            nc.vector.quantize_mx(out=zw[:].bitcast(FP8X4), scales=zs[:], in_=zq[c][:].rearrange("p j t -> p (j t)"))
-            groups = [(0, 2, "bank2"), (2, 4, "bank3")] if c == 3 else [(0, 4, ("bank7", "bank0", "bank1")[c])]
-            y_bank[c] = []
-            for lo, hi, tag in groups:
-                bank = psum.tile([P, hi - lo, CH], F32, name=tag)
+        value_banks = ([(0, 4, "bank7")], [(0, 4, "bank0")], [(0, 4, "bank1")], [(0, 2, "bank2"), (2, 4, "bank3")])
+
+        def second_product(c):
+            z_words = sb(f"z_words{c}", [P, CHUNK], U32)
+            z_scales = sb(f"z_scales{c}", [P, CHUNK], U8)
+            nc.vector.quantize_mx(out=z_words[:].bitcast(FP8X4), scales=z_scales[:], in_=z_rounded[c][:].rearrange("p j t -> p (j t)"))
+            y_banks[c] = []
+            for lo, hi, bank_name in value_banks[c]:
+                bank = psum.tile([P, hi - lo, CHUNK], F32, name=bank_name)
                 for t in range(lo, hi):
                     nc.tensor.matmul_mx(
                         out=bank[:, t - lo, :],
-                        lhsT=ww[:, t * P : (t + 1) * P].bitcast(FP8X4),
-                        lhsT_scale=wsc[:, t * P : (t + 1) * P],
-                        rhs=zw[:].bitcast(FP8X4),
-                        rhs_scale=zs[:],
+                        lhsT=values[:, t * P : (t + 1) * P].bitcast(FP8X4),
+                        lhsT_scale=value_scales[:, t * P : (t + 1) * P],
+                        rhs=z_words[:].bitcast(FP8X4),
+                        rhs_scale=z_scales[:],
                         start=True,
                         stop=True,
                     )
-                y_bank[c].append((lo, hi, bank))
+                y_banks[c].append((lo, hi, bank))
 
-        def result(c):
-            y = sb(f"y{c}", [P, PACK, CH], F32)
-            for lo, hi, bank in y_bank[c]:
-                nc.scalar.copy(y[:, lo:hi, :], bank[:])
-            nc.sync.dma_start(out_rows[:, :, c * CH : (c + 1) * CH], y[:])
-            y_sb[c] = y
+        def store_result(c):
+            y_sb[c] = sb(f"y{c}", [P, PACK, CHUNK], F32)
+            for lo, hi, bank in y_banks[c]:
+                nc.scalar.copy(y_sb[c][:, lo:hi, :], bank[:])
+            nc.sync.dma_start(out_planes[:, :, c * CHUNK : (c + 1) * CHUNK], y_sb[c][:])
 
-        def rounded(c):
-            yb = sb(f"yb{c}", [P, CH, PACK], BF16)
-            if c == 0:
-                nc.scalar.copy(yb[:], y_bank[c][0][2][:].rearrange("p t j -> p j t"))
-            else:
-                nc.vector.tensor_copy(yb[:].rearrange("p (c i) t -> p c t i", i=4), y_sb[c][:].rearrange("p t (c i) -> p c t i", i=4))
-            yb_sb[c] = yb
-
-        def planes(c):
-            nc.vector.quantize_mx(
-                out=yw[:, c * CH : (c + 1) * CH].bitcast(FP8X4),
-                scales=y_scales[:, c * CH : (c + 1) * CH],
-                in_=yb_sb[c][:].rearrange("p j t -> p (j t)"),
+        def round_result(c):
+            y_rounded[c] = sb(f"y_rounded{c}", [P, CHUNK, PACK], BF16)
+            nc.vector.tensor_copy(
+                y_rounded[c][:].rearrange("p (c i) t -> p c t i", i=LINE), y_sb[c][:].rearrange("p t (c i) -> p c t i", i=LINE)
             )
-            if c >= 2:
-                lo = 0 if c == 2 else c * CH
-                nc.sync.dma_start(out_words[:, lo : (c + 1) * CH], yw[:, lo : (c + 1) * CH])
 
-        tg_first = sb("tg_first", [P, CH], F32)
-        look_up(tg_first[:], 0, 0, CH)
-        queries(0)
-        first0 = scores("bank0", (0,), 0, CH)
-        s_first1 = ring.tile([P, 1, CH], F32, name="s_first1", offset=5 * TABLE, align_bytes=64)
-        nc.scalar.copy(s_first1[:], scores("bank1", (1,), 0, CH)[:])
-        s_first23 = ring.tile([P, 2, CH], F32, name="s_first23", offset=0, align_bytes=64)
-        nc.scalar.copy(s_first23[:], scores("bank2", (2, 3), 0, CH)[:])
-        queries(1)
-        deal_bytes(wsc, wsc_raw[:])
-        for r in range(1, 4):
-            nc.sync.dma_start(wsc_t[r:P:32, :].bitcast(I32), wsc_t[8 * r : P : 32, :].bitcast(I32))
-        tg_mid = ring.tile([P, 2 * CH], F32, name="tg_mid", offset=3 * TABLE, align_bytes=64)
-        look_up(tg_mid[:], 0, CH, 3 * CH)
-        mid0 = scores("bank3", (0,), CH, 3 * CH)
-        s_mid1 = sb("s_mid1", [P, 1, 2 * CH], F32)
-        nc.scalar.copy(s_mid1[:], scores("bank4", (1,), CH, 3 * CH)[:])
-        s_mid23 = sb("s_mid23", [P, 2, 2 * CH], F32)
-        nc.scalar.copy(s_mid23[:], scores("bank5", (2, 3), CH, 3 * CH)[:])
-        last = scores("bank6", range(PACK), 3 * CH, S)
+        def quantise_result(c):
+            nc.vector.quantize_mx(
+                out=y_words[:, c * CHUNK : (c + 1) * CHUNK].bitcast(FP8X4),
+                scales=y_scales[:, c * CHUNK : (c + 1) * CHUNK],
+                in_=y_rounded[c][:].rearrange("p j t -> p (j t)"),
+            )
 
-        u_first = sb("u_first", [P, PACK, CH], F32)
-        nc.vector.tensor_tensor(u_first[:, 0, :], first0[:, 0, :], tg_first[:], MULT)
-        fused(u_first[:, 1, :], 1, 0, CH, s_first1[:, 0, :])
+        mid_lo, last_lo = CHUNK, 3 * CHUNK
+
+        temp_first0 = sb("temp_first0", [P, CHUNK], F32)
+        look_up(temp_first0[:], 0, 0, mid_lo)
+        pick_queries(0, mid_lo)
+        bank_first0 = scores("bank0", (0,), 0, mid_lo)
+        s_first1 = work.tile([P, 1, CHUNK], F32, name="s_first1", offset=5 * SLOT, align_bytes=64)
+        nc.scalar.copy(s_first1[:], scores("bank1", (1,), 0, mid_lo)[:])
+        s_first23 = work.tile([P, 2, CHUNK], F32, name="s_first23", offset=0, align_bytes=64)
+        nc.scalar.copy(s_first23[:], scores("bank2", (2, 3), 0, mid_lo)[:])
+        pick_queries(mid_lo, S)
+        nc.vector.tensor_copy(
+            value_scales[:].rearrange("p (t m) -> p t m", t=PACK), w_scale_rows[:].rearrange("p (m t) -> p t m", t=PACK)
+        )
+        move_scale_rows(value_scales, (nc.sync, nc.sync, nc.sync))
+
+        temp_mid0 = work.tile([P, 2 * CHUNK], F32, name="temp_mid0", offset=3 * SLOT, align_bytes=64)
+        look_up(temp_mid0[:], 0, mid_lo, last_lo)
+        bank_mid0 = scores("bank3", (0,), mid_lo, last_lo)
+        s_mid1 = sb("s_mid1", [P, 1, 2 * CHUNK], F32)
+        nc.scalar.copy(s_mid1[:], scores("bank4", (1,), mid_lo, last_lo)[:])
+        s_mid23 = sb("s_mid23", [P, 2, 2 * CHUNK], F32)
+        nc.scalar.copy(s_mid23[:], scores("bank5", (2, 3), mid_lo, last_lo)[:])
+        bank_last = scores("bank6", range(PACK), last_lo, S)
+
+        u_first = sb("u_first", [P, PACK, CHUNK], F32)
+        nc.vector.tensor_tensor(u_first[:, 0, :], bank_first0[:, 0, :], temp_first0[:], MULT)
+        look_up_times(u_first[:, 1, :], 1, 0, mid_lo, s_first1[:, 0, :])
         for t in (2, 3):
-            fused(u_first[:, t, :], t, 0, CH, s_first23[:, t - 2, :])
-        u_sb[0] = u_first[:]
+            look_up_times(u_first[:, t, :], t, 0, mid_lo, s_first23[:, t - 2, :])
+        tempered[0] = u_first[:]
         squash(0)
 
-        u_mid = ring.tile([P, PACK, 2 * CH], F32, name="u_mid", offset=0, align_bytes=64)
-        nc.vector.tensor_tensor(u_mid[:, 0, :], mid0[:, 0, :], tg_mid[:], MULT)
-        fused(u_mid[:, 1, :], 1, CH, 3 * CH, s_mid1[:, 0, :])
+        u_mid = work.tile([P, PACK, 2 * CHUNK], F32, name="u_mid", offset=0, align_bytes=64)
+        nc.vector.tensor_tensor(u_mid[:, 0, :], bank_mid0[:, 0, :], temp_mid0[:], MULT)
+        look_up_times(u_mid[:, 1, :], 1, mid_lo, last_lo, s_mid1[:, 0, :])
         for t in (2, 3):
-            fused(u_mid[:, t, :], t, CH, 3 * CH, s_mid23[:, t - 2, :])
-        u_sb[1], u_sb[2] = u_mid[:, :, :CH], u_mid[:, :, CH:]
+            look_up_times(u_mid[:, t, :], t, mid_lo, last_lo, s_mid23[:, t - 2, :])
+        tempered[1], tempered[2] = u_mid[:, :, :CHUNK], u_mid[:, :, CHUNK:]
 
-        tg_last = ring.tile([P, PACK, CH], F32, name="tg_last", offset=5 * TABLE, align_bytes=64)
+        temp_last = work.tile([P, PACK, CHUNK], F32, name="temp_last", offset=5 * SLOT, align_bytes=64)
         for t in range(PACK):
-            look_up(tg_last[:, t, :], t, 3 * CH, S)
+            look_up(temp_last[:, t, :], t, last_lo, S)
         nc.scalar.copy(
-            ww[:].rearrange("p (t c i) -> p c t i", t=PACK, i=4), ww_raw[:].bitcast(U32).rearrange("p (c i t) -> p c t i", t=PACK, i=4)
+            values[:].rearrange("p (t c i) -> p c t i", t=PACK, i=LINE),
+            w_words[:].bitcast(U32).rearrange("p (c i t) -> p c t i", t=PACK, i=LINE),
         )
         gain(0)
-        u_last = sb("u_last", [P, PACK, CH], F32)
-        nc.vector.tensor_tensor(u_last[:], last[:], tg_last[:], MULT)
-        u_sb[3] = u_last[:]
+        u_last = sb("u_last", [P, PACK, CHUNK], F32)
+        nc.vector.tensor_tensor(u_last[:], bank_last[:], temp_last[:], MULT)
+        tempered[3] = u_last[:]
         for c in range(1, 4):
             squash(c)
-        values(0)
+
+        second_product(0)
         gain(1)
         gain(2)
-        values(1)
+        second_product(1)
         gain(3)
-        values(2)
-        values(3)
-        result(0)
-        rounded(0)
+        second_product(2)
+        second_product(3)
+        store_result(0)
+        y_rounded[0] = sb("y_rounded0", [P, CHUNK, PACK], BF16)
+        nc.scalar.copy(y_rounded[0][:], y_banks[0][0][2][:].rearrange("p t j -> p j t"))
         for c in range(1, 4):
-            result(c)
+            store_result(c)
         for c in range(1, 3):
-            rounded(c)
-            planes(c - 1)
-        planes(2)
-        rounded(3)
-        planes(3)
+            round_result(c)
+            quantise_result(c - 1)
+        quantise_result(2)
+        nc.sync.dma_start(out_words[:, :last_lo], y_words[:, :last_lo])
+        round_result(3)
+        quantise_result(3)
+        nc.sync.dma_start(out_words[:, last_lo:], y_words[:, last_lo:])
         for q in range(4):
-            eng = nc.scalar if q % 2 else nc.sync
-            eng.dma_start(out_2[0, 4 * q : 4 * q + 4, :].bitcast(I32), y_scales[32 * q : 32 * q + 4, :].bitcast(I32))
+            queue = nc.scalar if q % 2 else nc.sync
+            queue.dma_start(out_2[0, 4 * q : 4 * q + 4, :].bitcast(I32), y_scales[32 * q : 32 * q + 4, :].bitcast(I32))

@@ -143,17 +143,17 @@ def tile_picked_temper_tanh_po_kernel(
         tempered, squashed, z_rounded, y_banks, y_sb, y_rounded = {}, {}, {}, {}, {}, {}
 
         def squash(c):
-            squashed[c] = sb(f"squashed{c}", [P, CHUNK, PACK], F32)
-            nc.scalar.activation(
-                squashed[c][:].rearrange("p (c i) t -> p c t i", i=LINE),
-                tempered[c].rearrange("p t (c i) -> p c t i", i=LINE),
-                ACT.Tanh,
-                scale=0.0625,
-            )
+            squashed[c] = sb(f"squashed{c}", [P, PACK, CHUNK], F32)
+            nc.scalar.activation(squashed[c][:], tempered[c], ACT.Tanh, scale=0.0625)
 
-        def gain(c):
-            z_rounded[c] = sb(f"z_rounded{c}", [P, CHUNK, PACK], BF16)
-            nc.vector.tensor_tensor(z_rounded[c][:], squashed[c][:], gn_sb[:].unsqueeze(1).to_broadcast([P, CHUNK, PACK]), MULT)
+        def gain(c, out):
+            nc.vector.tensor_tensor(
+                out[:].rearrange("p (c i) t -> p c t i", i=LINE),
+                squashed[c][:].rearrange("p t (c i) -> p c t i", i=LINE),
+                gn_sb[:].unsqueeze(1).unsqueeze(3).to_broadcast([P, CHUNK // LINE, PACK, LINE]),
+                MULT,
+            )
+            z_rounded[c] = out
 
         value_banks = ([(0, 4, "bank7")], [(0, 4, "bank0")], [(0, 4, "bank1")], [(0, 2, "bank2"), (2, 4, "bank3")])
 
@@ -242,7 +242,7 @@ def tile_picked_temper_tanh_po_kernel(
             values[:].rearrange("p (t c i) -> p c t i", t=PACK, i=LINE),
             w_words[:].bitcast(U32).rearrange("p (c i t) -> p c t i", t=PACK, i=LINE),
         )
-        gain(0)
+        gain(0, sb("z_rounded0", [P, CHUNK, PACK], BF16))
         u_last = sb("u_last", [P, PACK, CHUNK], F32)
         nc.vector.tensor_tensor(u_last[:], bank_last[:], temp_last[:], MULT)
         tempered[3] = u_last[:]
@@ -250,23 +250,20 @@ def tile_picked_temper_tanh_po_kernel(
             squash(c)
 
         second_product(0)
-        gain(1)
-        gain(2)
+        gain(1, work.tile([P, CHUNK, PACK], BF16, name="z_rounded1", offset=7 * SLOT, align_bytes=64))
+        gain(2, sb("z_rounded2", [P, CHUNK, PACK], BF16))
         second_product(1)
-        gain(3)
         second_product(2)
-        second_product(3)
+        gain(3, work.tile([P, CHUNK, PACK], BF16, name="z_rounded3", offset=7 * SLOT, align_bytes=64))
         store_result(0)
-        y_rounded[0] = sb("y_rounded0", [P, CHUNK, PACK], BF16)
-        nc.scalar.copy(y_rounded[0][:], y_banks[0][0][2][:].rearrange("p t j -> p j t"))
+        round_result(0)
+        second_product(3)
         for c in range(1, 4):
             store_result(c)
-        for c in range(1, 3):
+        for c in range(1, 4):
             round_result(c)
             quantise_result(c - 1)
-        quantise_result(2)
         nc.sync.dma_start(out_words[:, :last_lo], y_words[:, :last_lo])
-        round_result(3)
         quantise_result(3)
         nc.sync.dma_start(out_words[:, last_lo:], y_words[:, last_lo:])
         for q in range(4):

@@ -19,6 +19,7 @@ S = 512
 CHUNK = 128
 HALF = S // 2
 LINE = 4
+RUN = 4
 SLOT = 2048
 FLOPS = 2 * 2 * 512 * 512 * 512
 
@@ -53,25 +54,39 @@ def tile_picked_temper_tanh_po_kernel(
         task_sb = sb("task_sb", [P, S // 16], U16)
         d_scale_table = sb("d_scale_table", [P, TABLE], U8)
         x_scale_table = sb("x_scale_table", [P, TABLE], U8)
-        w_scale_rows = work.tile([P, S], U8, name="w_scale_rows", offset=3 * SLOT, align_bytes=64)
+        w_scale_rows = sb("w_scale_rows", [P, S], U8)
         d_word_table = loads.tile([P, TABLE], I32, name="d_word_table", offset=4 * SLOT)
-        x_word_table = loads.tile([P, TABLE], I32, name="x_word_table", offset=8 * SLOT, align_bytes=64)
+        x_word_table = sb("x_word_table", [P, TABLE], I32)
         for rows in (d_scale_table, x_scale_table, w_scale_rows):
             nc.vector.memset(rows[:].bitcast(I32), 0)
+        temp_planes = temp.rearrange("(p t) u -> p t u", t=PACK)
+        temp_sb = [sb("temp0", [P, S], F32)]
         nc.sync.dma_start(kidx_sb[:], kidx)
         nc.sync.dma_start(offs_sb[:], offs)
         nc.sync.dma_start(d_scale_table[0:P:8, :].bitcast(I32), d_scales[0].bitcast(I32))
         nc.sync.dma_start(task_sb[:], task)
         nc.sync.dma_start(x_scale_table[0:P:8, :].bitcast(I32), x_scales[0].bitcast(I32))
+        nc.sync.dma_start(temp_sb[0][:], temp_planes[:, 0, :])
+        nc.sync.dma_start(w_scale_rows[0:P:8, :].bitcast(I32), w1_scales[0].bitcast(I32))
         nc.sync.dma_start(d_word_table[:], words_of(d_words))
         nc.sync.dma_start(x_word_table[:], words_of(x_words))
-        nc.sync.dma_start(w_scale_rows[0:P:8, :].bitcast(I32), w1_scales[0].bitcast(I32))
-        temp_planes = temp.rearrange("(p t) u -> p t u", t=PACK)
-        temp_sb = [sb("temp0", [P, S], F32)]
-        nc.sync.dma_start(temp_sb[0][:], temp_planes[:, 0, :])
 
-        score_scales = sb("score_scales", [P, 2 * S], U8)
-        key_scales, query_scales = score_scales[:, :S], score_scales[:, S:]
+        def look_up(out, t, lo, hi):
+            nc.scalar.activation(out, temp_sb[t][:].indirect(entries(task_sb, lo, hi)), ACT.Copy)
+
+        def look_up_times(out, t, lo, hi, copied_scores):
+            nc.vector.tensor_tensor(out, temp_sb[t][:].indirect(entries(task_sb, lo, hi)), copied_scores, MULT)
+
+        mid_lo, last_lo = CHUNK, 3 * CHUNK
+        temp_first0 = sb("temp_first0", [P, CHUNK], F32)
+        temp_rest0 = sb("temp_rest0", [P, 3 * CHUNK], F32)
+        look_up(temp_first0[:], 0, 0, mid_lo)
+        look_up(temp_rest0[:, : 2 * CHUNK], 0, mid_lo, last_lo)
+        look_up(temp_rest0[:, 2 * CHUNK :], 0, last_lo, S)
+
+        scales = sb("scales", [P, 2 * S], U8)
+        key_scales, query_scales = scales[:, :S], scales[:, S:]
+        value_scales = sb("value_scales", [P, S], U8)
         d_scales_picked = sb("d_scales_picked", [P, S], U8)
         for h in range(2):
             nc.vector.tensor_copy(
@@ -85,7 +100,8 @@ def tile_picked_temper_tanh_po_kernel(
                 d_scales_picked[:].rearrange("p (h m t) -> p h t m", t=PACK, h=2)[:, h],
             )
         nc.vector.tensor_copy(query_scales.bitcast(I32), x_scales_picked[:].bitcast(I32))
-        move_scale_rows(score_scales, (nc.sync, nc.scalar, nc.sync))
+        move_scale_rows(scales, (nc.sync, nc.scalar, nc.sync))
+        nc.vector.tensor_copy(value_scales[:].rearrange("p (t m) -> p t m", t=PACK), w_scale_rows[:].rearrange("p (m t) -> p t m", t=PACK))
 
         d_words_picked = sb("d_words_picked", [P, S], U32)
         keys = sb("keys", [P, S], U32)
@@ -109,36 +125,35 @@ def tile_picked_temper_tanh_po_kernel(
         gn_sb = loads.tile([P, PACK], F32, name="gn_sb", offset=5 * SLOT)
         nc.sync.dma_start(gn_sb[:], gn.rearrange("(p t) o -> p (t o)", t=PACK))
 
-        queries = sb("queries", [P, S], U32)
+        move_scale_rows(value_scales, (nc.sync, nc.sync, nc.sync))
+
+        queries_first = work.tile([P, CHUNK], U32, name="queries_first", offset=0, align_bytes=64)
+        queries_rest = sb("queries_rest", [P, 3 * CHUNK], U32)
         values = sb("values", [P, S], U32)
-        value_scales = loads.tile([P, S], U8, name="value_scales", offset=9 * SLOT, align_bytes=64)
         y_scales = sb("y_scales", [P, S], U8)
         y_words = sb("y_words", [P, S], I32)
         out_planes = out_0.rearrange("(p t) j -> p t j", t=PACK)
         out_words = words_of(out_1)
 
-        def pick_queries(lo, hi):
-            nc.vector.tensor_copy(queries[:, lo:hi], x_word_table[:].bitcast(U32).indirect(entries(offs_sb, lo, hi)))
+        def pick_queries(out, lo, hi):
+            nc.vector.tensor_copy(out, x_word_table[:].bitcast(U32).indirect(entries(offs_sb, lo, hi)))
 
-        def scores(bank_name, planes, lo, hi):
+        def score_pass(out, t, picked, lo, hi):
+            nc.tensor.matmul_mx(
+                out=out,
+                lhsT=keys[:, t * P : (t + 1) * P].bitcast(FP8X4),
+                lhsT_scale=key_scales[:, t * P : (t + 1) * P],
+                rhs=picked.bitcast(FP8X4),
+                rhs_scale=query_scales[:, lo:hi],
+                start=True,
+                stop=True,
+            )
+
+        def scores(bank_name, planes, picked, lo, hi):
             bank = psum.tile([P, len(planes), hi - lo], F32, name=bank_name)
             for e, t in enumerate(planes):
-                nc.tensor.matmul_mx(
-                    out=bank[:, e, :],
-                    lhsT=keys[:, t * P : (t + 1) * P].bitcast(FP8X4),
-                    lhsT_scale=key_scales[:, t * P : (t + 1) * P],
-                    rhs=queries[:, lo:hi].bitcast(FP8X4),
-                    rhs_scale=query_scales[:, lo:hi],
-                    start=True,
-                    stop=True,
-                )
+                score_pass(bank[:, e, :], t, picked, lo, hi)
             return bank
-
-        def look_up(out, t, lo, hi):
-            nc.scalar.activation(out, temp_sb[t][:].indirect(entries(task_sb, lo, hi)), ACT.Copy)
-
-        def look_up_times(out, t, lo, hi, copied_scores):
-            nc.vector.tensor_tensor(out, temp_sb[t][:].indirect(entries(task_sb, lo, hi)), copied_scores, MULT)
 
         tempered, squashed, z_rounded, y_banks, y_sb, y_rounded = {}, {}, {}, {}, {}, {}
 
@@ -148,9 +163,9 @@ def tile_picked_temper_tanh_po_kernel(
 
         def gain(c, out):
             nc.vector.tensor_tensor(
-                out[:].rearrange("p (c i) t -> p c t i", i=LINE),
-                squashed[c][:].rearrange("p t (c i) -> p c t i", i=LINE),
-                gn_sb[:].unsqueeze(1).unsqueeze(3).to_broadcast([P, CHUNK // LINE, PACK, LINE]),
+                out[:].rearrange("p (c i) t -> p c t i", i=RUN),
+                squashed[c][:].rearrange("p t (c i) -> p c t i", i=RUN),
+                gn_sb[:].unsqueeze(1).unsqueeze(3).to_broadcast([P, CHUNK // RUN, PACK, RUN]),
                 MULT,
             )
             z_rounded[c] = out
@@ -185,7 +200,7 @@ def tile_picked_temper_tanh_po_kernel(
         def round_result(c):
             y_rounded[c] = sb(f"y_rounded{c}", [P, CHUNK, PACK], BF16)
             nc.vector.tensor_copy(
-                y_rounded[c][:].rearrange("p (c i) t -> p c t i", i=LINE), y_sb[c][:].rearrange("p t (c i) -> p c t i", i=LINE)
+                y_rounded[c][:].rearrange("p (c i) t -> p c t i", i=RUN), y_sb[c][:].rearrange("p t (c i) -> p c t i", i=RUN)
             )
 
         def quantise_result(c):
@@ -195,57 +210,54 @@ def tile_picked_temper_tanh_po_kernel(
                 in_=y_rounded[c][:].rearrange("p j t -> p (j t)"),
             )
 
-        mid_lo, last_lo = CHUNK, 3 * CHUNK
+        pick_queries(queries_first[:], 0, mid_lo)
+        bank_first0 = scores("bank0", (0,), queries_first[:], 0, mid_lo)
+        s_first1 = sb("s_first1", [P, 1, CHUNK], F32)
+        nc.scalar.copy(s_first1[:], scores("bank1", (1,), queries_first[:], 0, mid_lo)[:])
+        s_first23 = work.tile([P, 2, CHUNK], F32, name="s_first23", offset=2 * SLOT, align_bytes=64)
+        nc.scalar.copy(s_first23[:], scores("bank2", (2, 3), queries_first[:], 0, mid_lo)[:])
+        pick_queries(queries_rest[:], mid_lo, S)
+        queries_mid, queries_last = queries_rest[:, : 2 * CHUNK], queries_rest[:, 2 * CHUNK :]
 
-        temp_first0 = sb("temp_first0", [P, CHUNK], F32)
-        look_up(temp_first0[:], 0, 0, mid_lo)
-        pick_queries(0, mid_lo)
-        bank_first0 = scores("bank0", (0,), 0, mid_lo)
-        s_first1 = work.tile([P, 1, CHUNK], F32, name="s_first1", offset=5 * SLOT, align_bytes=64)
-        nc.scalar.copy(s_first1[:], scores("bank1", (1,), 0, mid_lo)[:])
-        s_first23 = work.tile([P, 2, CHUNK], F32, name="s_first23", offset=0, align_bytes=64)
-        nc.scalar.copy(s_first23[:], scores("bank2", (2, 3), 0, mid_lo)[:])
-        pick_queries(mid_lo, S)
-        nc.vector.tensor_copy(
-            value_scales[:].rearrange("p (t m) -> p t m", t=PACK), w_scale_rows[:].rearrange("p (m t) -> p t m", t=PACK)
-        )
-        move_scale_rows(value_scales, (nc.sync, nc.sync, nc.sync))
+        def scores_rest(bank_name, t):
+            bank = psum.tile([P, 3 * CHUNK], F32, name=bank_name)
+            score_pass(bank[:, : 2 * CHUNK], t, queries_mid, mid_lo, last_lo)
+            score_pass(bank[:, 2 * CHUNK :], t, queries_last, last_lo, S)
+            return bank
 
-        temp_mid0 = work.tile([P, 2 * CHUNK], F32, name="temp_mid0", offset=3 * SLOT, align_bytes=64)
-        look_up(temp_mid0[:], 0, mid_lo, last_lo)
-        bank_mid0 = scores("bank3", (0,), mid_lo, last_lo)
-        s_mid1 = sb("s_mid1", [P, 1, 2 * CHUNK], F32)
-        nc.scalar.copy(s_mid1[:], scores("bank4", (1,), mid_lo, last_lo)[:])
-        s_mid23 = sb("s_mid23", [P, 2, 2 * CHUNK], F32)
-        nc.scalar.copy(s_mid23[:], scores("bank5", (2, 3), mid_lo, last_lo)[:])
-        bank_last = scores("bank6", range(PACK), last_lo, S)
+        bank_rest0 = scores_rest("bank3", 0)
+        bank_mid12 = scores("bank4", (1, 2), queries_mid, mid_lo, last_lo)
+        bank_mid3 = scores("bank5", (3,), queries_mid, mid_lo, last_lo)
+        bank_last = scores("bank6", (1, 2, 3), queries_last, last_lo, S)
+        temp_mid12 = work.tile([P, 2, 2 * CHUNK], F32, name="temp_mid12", offset=0, align_bytes=64)
+        temp_last = work.tile([P, 3, CHUNK], F32, name="temp_last", offset=6 * SLOT, align_bytes=64)
+        s_mid3 = work.tile([P, 2 * CHUNK], F32, name="s_mid3", offset=7 * SLOT // 4, align_bytes=64)
 
-        u_first = sb("u_first", [P, PACK, CHUNK], F32)
+        u_first = work.tile([P, PACK, CHUNK], F32, name="u_first", offset=6 * SLOT, align_bytes=64)
         nc.vector.tensor_tensor(u_first[:, 0, :], bank_first0[:, 0, :], temp_first0[:], MULT)
         look_up_times(u_first[:, 1, :], 1, 0, mid_lo, s_first1[:, 0, :])
         for t in (2, 3):
             look_up_times(u_first[:, t, :], t, 0, mid_lo, s_first23[:, t - 2, :])
         tempered[0] = u_first[:]
+        for t in (1, 2):
+            look_up(temp_mid12[:, t - 1, :], t, mid_lo, last_lo)
         squash(0)
+        nc.scalar.copy(s_mid3[:], bank_mid3[:, 0, :])
+        for t in (1, 2, 3):
+            look_up(temp_last[:, t - 1, :], t, last_lo, S)
 
-        u_mid = work.tile([P, PACK, 2 * CHUNK], F32, name="u_mid", offset=0, align_bytes=64)
-        nc.vector.tensor_tensor(u_mid[:, 0, :], bank_mid0[:, 0, :], temp_mid0[:], MULT)
-        look_up_times(u_mid[:, 1, :], 1, mid_lo, last_lo, s_mid1[:, 0, :])
-        for t in (2, 3):
-            look_up_times(u_mid[:, t, :], t, mid_lo, last_lo, s_mid23[:, t - 2, :])
-        tempered[1], tempered[2] = u_mid[:, :, :CHUNK], u_mid[:, :, CHUNK:]
-
-        temp_last = work.tile([P, PACK, CHUNK], F32, name="temp_last", offset=5 * SLOT, align_bytes=64)
-        for t in range(PACK):
-            look_up(temp_last[:, t, :], t, last_lo, S)
+        u_rest = work.tile([P, PACK, 3 * CHUNK], F32, name="u_rest", offset=9 * SLOT // 4, align_bytes=64)
+        nc.vector.tensor_tensor(u_rest[:, 0, :], bank_rest0[:], temp_rest0[:], MULT)
+        nc.vector.tensor_tensor(u_rest[:, 1:3, : 2 * CHUNK], bank_mid12[:], temp_mid12[:], MULT)
+        look_up_times(u_rest[:, 3, : 2 * CHUNK], 3, mid_lo, last_lo, s_mid3[:])
+        gain(0, sb("z_rounded0", [P, CHUNK, PACK], BF16))
+        nc.vector.tensor_tensor(u_rest[:, 1:, 2 * CHUNK :], bank_last[:], temp_last[:], MULT)
+        for c in range(1, 4):
+            tempered[c] = u_rest[:, :, (c - 1) * CHUNK : c * CHUNK]
         nc.scalar.copy(
             values[:].rearrange("p (t c i) -> p c t i", t=PACK, i=LINE),
             w_words[:].bitcast(U32).rearrange("p (c i t) -> p c t i", t=PACK, i=LINE),
         )
-        gain(0, sb("z_rounded0", [P, CHUNK, PACK], BF16))
-        u_last = sb("u_last", [P, PACK, CHUNK], F32)
-        nc.vector.tensor_tensor(u_last[:], bank_last[:], temp_last[:], MULT)
-        tempered[3] = u_last[:]
         for c in range(1, 4):
             squash(c)
 

@@ -19,7 +19,7 @@ S = 512
 CHUNK = 128
 HALF = S // 2
 LINE = 4
-RUN = 4
+RUN = 2
 SLOT = 2048
 FLOPS = 2 * 2 * 512 * 512 * 512
 
@@ -63,12 +63,12 @@ def tile_picked_temper_tanh_po_kernel(
         temp_sb = [sb("temp0", [P, S], F32)]
         nc.sync.dma_start(kidx_sb[:], kidx)
         nc.sync.dma_start(offs_sb[:], offs)
-        nc.sync.dma_start(d_scale_table[0:P:8, :].bitcast(I32), d_scales[0].bitcast(I32))
         nc.sync.dma_start(task_sb[:], task)
-        nc.sync.dma_start(x_scale_table[0:P:8, :].bitcast(I32), x_scales[0].bitcast(I32))
+        nc.sync.dma_start(d_scale_table[0:P:8, :].bitcast(I32), d_scales[0].bitcast(I32))
         nc.sync.dma_start(temp_sb[0][:], temp_planes[:, 0, :])
-        nc.sync.dma_start(w_scale_rows[0:P:8, :].bitcast(I32), w1_scales[0].bitcast(I32))
+        nc.sync.dma_start(x_scale_table[0:P:8, :].bitcast(I32), x_scales[0].bitcast(I32))
         nc.sync.dma_start(d_word_table[:], words_of(d_words))
+        nc.sync.dma_start(w_scale_rows[0:P:8, :].bitcast(I32), w1_scales[0].bitcast(I32))
         nc.sync.dma_start(x_word_table[:], words_of(x_words))
 
         def look_up(out, t, lo, hi):
@@ -199,9 +199,8 @@ def tile_picked_temper_tanh_po_kernel(
 
         def round_result(c):
             y_rounded[c] = sb(f"y_rounded{c}", [P, CHUNK, PACK], BF16)
-            nc.vector.tensor_copy(
-                y_rounded[c][:].rearrange("p (c i) t -> p c t i", i=RUN), y_sb[c][:].rearrange("p t (c i) -> p c t i", i=RUN)
-            )
+            copy = nc.scalar.copy if c == 0 else nc.vector.tensor_copy
+            copy(y_rounded[c][:].rearrange("p (c i) t -> p c t i", i=RUN), y_sb[c][:].rearrange("p t (c i) -> p c t i", i=RUN))
 
         def quantise_result(c):
             nc.vector.quantize_mx(
@@ -254,9 +253,9 @@ def tile_picked_temper_tanh_po_kernel(
         nc.vector.tensor_tensor(u_rest[:, 1:, 2 * CHUNK :], bank_last[:], temp_last[:], MULT)
         for c in range(1, 4):
             tempered[c] = u_rest[:, :, (c - 1) * CHUNK : c * CHUNK]
-        nc.scalar.copy(
-            values[:].rearrange("p (t c i) -> p c t i", t=PACK, i=LINE),
-            w_words[:].bitcast(U32).rearrange("p (c i t) -> p c t i", t=PACK, i=LINE),
+        nc.vector.tensor_copy(
+            values[:].bitcast(I32).rearrange("p (t c i) -> p c t i", t=PACK, i=LINE),
+            w_words[:].rearrange("p (c i t) -> p c t i", t=PACK, i=LINE),
         )
         for c in range(1, 4):
             squash(c)
@@ -269,15 +268,17 @@ def tile_picked_temper_tanh_po_kernel(
         gain(3, work.tile([P, CHUNK, PACK], BF16, name="z_rounded3", offset=7 * SLOT, align_bytes=64))
         store_result(0)
         round_result(0)
+        quantise_result(0)
+        nc.sync.dma_start(out_words[:, :CHUNK], y_words[:, :CHUNK])
         second_product(3)
         for c in range(1, 4):
             store_result(c)
-        for c in range(1, 4):
+        round_result(1)
+        for c in range(2, 4):
             round_result(c)
             quantise_result(c - 1)
-        nc.sync.dma_start(out_words[:, :last_lo], y_words[:, :last_lo])
         quantise_result(3)
-        nc.sync.dma_start(out_words[:, last_lo:], y_words[:, last_lo:])
+        nc.sync.dma_start(out_words[:, CHUNK:], y_words[:, CHUNK:])
         for q in range(4):
             queue = nc.scalar if q % 2 else nc.sync
             queue.dma_start(out_2[0, 4 * q : 4 * q + 4, :].bitcast(I32), y_scales[32 * q : 32 * q + 4, :].bitcast(I32))

@@ -38,15 +38,14 @@ def tile_picked_temper_tanh_po_kernel(
     nc = tc.nc
     with ExitStack() as ctx:
         keep = ctx.enter_context(tc.tile_pool(name="keep", bufs=1))
-        work = ctx.enter_context(tc.tile_pool(name="work", bufs=1))
         loads = ctx.enter_context(tc.tile_pool(name="loads", bufs=1))
         psum = ctx.enter_context(tc.psum_pool(name="psum", bufs=1))
 
         def sb(name, shape, dtype):
             return keep.tile(shape, dtype, name=name, align_bytes=64)
 
-        def move_scale_rows(tile, queues):
-            for r, queue in zip(range(1, PACK), queues):
+        def move_scale_rows(tile, queue):
+            for r in range(1, PACK):
                 queue.dma_start(tile[r:P:32, :].bitcast(I32), tile[8 * r : P : 32, :].bitcast(I32))
 
         kidx_sb = sb("kidx_sb", [P, S // 16], U16)
@@ -55,79 +54,64 @@ def tile_picked_temper_tanh_po_kernel(
         d_scale_table = sb("d_scale_table", [P, TABLE], U8)
         x_scale_table = sb("x_scale_table", [P, TABLE], U8)
         w_scale_rows = sb("w_scale_rows", [P, S], U8)
-        d_word_table = loads.tile([P, TABLE], I32, name="d_word_table", offset=4 * SLOT)
+        d_word_table = loads.tile([P, TABLE], I32, name="d_word_table", offset=0)
         x_word_table = sb("x_word_table", [P, TABLE], I32)
         for rows in (d_scale_table, x_scale_table, w_scale_rows):
             nc.vector.memset(rows[:].bitcast(I32), 0)
         temp_planes = temp.rearrange("(p t) u -> p t u", t=PACK)
-        temp_sb = [sb("temp0", [P, S], F32)]
+        temp_sb = [sb(f"temp{t}", [P, S], F32) for t in range(PACK)]
+        nc.sync.dma_start(temp_sb[0][:], temp_planes[:, 0, :])
         nc.sync.dma_start(kidx_sb[:], kidx)
         nc.sync.dma_start(offs_sb[:], offs)
         nc.sync.dma_start(task_sb[:], task)
         nc.sync.dma_start(d_scale_table[0:P:8, :].bitcast(I32), d_scales[0].bitcast(I32))
-        nc.sync.dma_start(temp_sb[0][:], temp_planes[:, 0, :])
+        nc.sync.dma_start(temp_sb[1][:], temp_planes[:, 1, :])
         nc.sync.dma_start(x_scale_table[0:P:8, :].bitcast(I32), x_scales[0].bitcast(I32))
         nc.sync.dma_start(d_word_table[:], words_of(d_words))
         nc.sync.dma_start(w_scale_rows[0:P:8, :].bitcast(I32), w1_scales[0].bitcast(I32))
+        nc.sync.dma_start(temp_sb[2][:], temp_planes[:, 2, :])
         nc.sync.dma_start(x_word_table[:], words_of(x_words))
+        nc.sync.dma_start(temp_sb[3][:], temp_planes[:, 3, :])
 
-        def look_up(out, t, lo, hi):
-            nc.scalar.activation(out, temp_sb[t][:].indirect(entries(task_sb, lo, hi)), ACT.Copy)
+        temp_picked = sb("temp_picked", [P, PACK, S], F32)
 
-        def look_up_times(out, t, lo, hi, copied_scores):
-            nc.vector.tensor_tensor(out, temp_sb[t][:].indirect(entries(task_sb, lo, hi)), copied_scores, MULT)
+        def look_up(t, lo, hi):
+            nc.scalar.activation(temp_picked[:, t, lo:hi], temp_sb[t][:].indirect(entries(task_sb, lo, hi)), ACT.Copy)
 
-        mid_lo, last_lo = CHUNK, 3 * CHUNK
-        temp_first0 = sb("temp_first0", [P, CHUNK], F32)
-        temp_rest0 = sb("temp_rest0", [P, 3 * CHUNK], F32)
-        look_up(temp_first0[:], 0, 0, mid_lo)
-        look_up(temp_rest0[:, : 2 * CHUNK], 0, mid_lo, last_lo)
-        look_up(temp_rest0[:, 2 * CHUNK :], 0, last_lo, S)
+        for t in range(2):
+            look_up(t, 0, HALF)
+            look_up(t, HALF, S)
 
         scales = sb("scales", [P, 2 * S], U8)
         key_scales, query_scales = scales[:, :S], scales[:, S:]
         value_scales = sb("value_scales", [P, S], U8)
         d_scales_picked = sb("d_scales_picked", [P, S], U8)
-        for h in range(2):
-            nc.vector.tensor_copy(
-                d_scales_picked[:, h * HALF : (h + 1) * HALF], d_scale_table[:].indirect(entries(kidx_sb, h * HALF, (h + 1) * HALF))
-            )
-        x_scales_picked = loads.tile([P, S], U8, name="x_scales_picked", offset=SLOT - S // 2)
+        x_scales_picked = sb("x_scales_picked", [P, S], U8)
+        nc.vector.tensor_copy(d_scales_picked[:], d_scale_table[:].indirect(kidx_sb[:]))
         nc.vector.tensor_copy(x_scales_picked[:], x_scale_table[:].indirect(offs_sb[:]))
-        for h in range(2):
-            nc.vector.tensor_copy(
-                key_scales.rearrange("p (t h m) -> p h t m", t=PACK, h=2)[:, h],
-                d_scales_picked[:].rearrange("p (h m t) -> p h t m", t=PACK, h=2)[:, h],
-            )
+        nc.vector.tensor_copy(
+            key_scales.rearrange("p (t m) -> p t m", t=PACK), d_scales_picked[:].rearrange("p (m t) -> p t m", t=PACK)
+        )
         nc.vector.tensor_copy(query_scales.bitcast(I32), x_scales_picked[:].bitcast(I32))
-        move_scale_rows(scales, (nc.sync, nc.scalar, nc.sync))
-        nc.vector.tensor_copy(value_scales[:].rearrange("p (t m) -> p t m", t=PACK), w_scale_rows[:].rearrange("p (m t) -> p t m", t=PACK))
+        move_scale_rows(scales, nc.scalar)
+        look_up(2, 0, HALF)
+        look_up(2, HALF, S)
 
         d_words_picked = sb("d_words_picked", [P, S], U32)
         keys = sb("keys", [P, S], U32)
-        for h in range(2):
-            nc.vector.tensor_copy(
-                d_words_picked[:, h * HALF : (h + 1) * HALF],
-                d_word_table[:].bitcast(U32).indirect(entries(kidx_sb, h * HALF, (h + 1) * HALF)),
-            )
-        for h in range(2):
-            nc.vector.tensor_copy(
-                keys[:].bitcast(I32).rearrange("p (t h c i) -> p h c t i", t=PACK, h=2, i=LINE)[:, h],
-                d_words_picked[:].bitcast(I32).rearrange("p (h c i t) -> p h c t i", t=PACK, h=2, i=LINE)[:, h],
-            )
-
-        for t, slot in ((1, 0), (2, 1), (3, 6)):
-            plane = loads.tile([P, S], F32, name=f"temp{t}", offset=slot * SLOT)
-            nc.sync.dma_start(plane[:], temp_planes[:, t, :])
-            temp_sb.append(plane)
-        w_words = loads.tile([P, S], I32, name="w_words", offset=4 * SLOT)
+        nc.vector.tensor_copy(d_words_picked[:], d_word_table[:].bitcast(U32).indirect(kidx_sb[:]))
+        nc.vector.tensor_copy(value_scales[:].rearrange("p (t m) -> p t m", t=PACK), w_scale_rows[:].rearrange("p (m t) -> p t m", t=PACK))
+        nc.vector.tensor_copy(
+            keys[:].bitcast(I32).rearrange("p (t c i) -> p c t i", t=PACK, i=LINE),
+            d_words_picked[:].bitcast(I32).rearrange("p (c i t) -> p c t i", t=PACK, i=LINE),
+        )
+        w_words = loads.tile([P, S], I32, name="w_words", offset=SLOT + 64)
         nc.sync.dma_start(w_words[:], words_of(w1_words))
-        gn_sb = loads.tile([P, PACK], F32, name="gn_sb", offset=5 * SLOT)
+        gn_sb = loads.tile([P, PACK], F32, name="gn_sb", offset=SLOT)
         nc.sync.dma_start(gn_sb[:], gn.rearrange("(p t) o -> p (t o)", t=PACK))
+        move_scale_rows(value_scales, nc.sync)
 
-        move_scale_rows(value_scales, (nc.sync, nc.sync, nc.sync))
-
-        queries_first = work.tile([P, CHUNK], U32, name="queries_first", offset=0, align_bytes=64)
+        queries_first = sb("queries_first", [P, CHUNK], U32)
         queries_rest = sb("queries_rest", [P, 3 * CHUNK], U32)
         values = sb("values", [P, S], U32)
         y_scales = sb("y_scales", [P, S], U8)
@@ -138,145 +122,102 @@ def tile_picked_temper_tanh_po_kernel(
         def pick_queries(out, lo, hi):
             nc.vector.tensor_copy(out, x_word_table[:].bitcast(U32).indirect(entries(offs_sb, lo, hi)))
 
-        def score_pass(out, t, picked, lo, hi):
-            nc.tensor.matmul_mx(
-                out=out,
-                lhsT=keys[:, t * P : (t + 1) * P].bitcast(FP8X4),
-                lhsT_scale=key_scales[:, t * P : (t + 1) * P],
-                rhs=picked.bitcast(FP8X4),
-                rhs_scale=query_scales[:, lo:hi],
-                start=True,
-                stop=True,
-            )
-
-        def scores(bank_name, planes, picked, lo, hi):
-            bank = psum.tile([P, len(planes), hi - lo], F32, name=bank_name)
+        def product(bank_name, stationary, stationary_scales, moving, moving_scales, planes):
+            bank = psum.tile([P, len(planes), CHUNK], F32, name=bank_name)
             for e, t in enumerate(planes):
-                score_pass(bank[:, e, :], t, picked, lo, hi)
+                nc.tensor.matmul_mx(
+                    out=bank[:, e, :],
+                    lhsT=stationary[:, t * P : (t + 1) * P].bitcast(FP8X4),
+                    lhsT_scale=stationary_scales[:, t * P : (t + 1) * P],
+                    rhs=moving.bitcast(FP8X4),
+                    rhs_scale=moving_scales,
+                    start=True,
+                    stop=True,
+                )
             return bank
 
-        tempered, squashed, z_rounded, y_banks, y_sb, y_rounded = {}, {}, {}, {}, {}, {}
+        def columns(c):
+            return slice(c * CHUNK, (c + 1) * CHUNK)
+
+        scores, tempered, squashed, z_rounded, y_banks, y_sb, y_rounded = {}, {}, {}, {}, {}, {}, {}
+
+        def temper(c):
+            tempered[c] = sb(f"tempered{c}", [P, PACK, CHUNK], F32)
+            nc.vector.tensor_tensor(tempered[c][:], scores[c][:], temp_picked[:, :, columns(c)], MULT)
 
         def squash(c):
             squashed[c] = sb(f"squashed{c}", [P, PACK, CHUNK], F32)
-            nc.scalar.activation(squashed[c][:], tempered[c], ACT.Tanh, scale=0.0625)
+            nc.scalar.activation(squashed[c][:], tempered[c][:], ACT.Tanh, scale=0.0625)
 
-        def gain(c, out):
+        def gain(c):
+            z_rounded[c] = sb(f"z_rounded{c}", [P, CHUNK, PACK], BF16)
             nc.vector.tensor_tensor(
-                out[:].rearrange("p (c i) t -> p c t i", i=RUN),
+                z_rounded[c][:].rearrange("p (c i) t -> p c t i", i=RUN),
                 squashed[c][:].rearrange("p t (c i) -> p c t i", i=RUN),
                 gn_sb[:].unsqueeze(1).unsqueeze(3).to_broadcast([P, CHUNK // RUN, PACK, RUN]),
                 MULT,
             )
-            z_rounded[c] = out
 
-        value_banks = ([(0, 4, "bank7")], [(0, 4, "bank0")], [(0, 4, "bank1")], [(0, 2, "bank2"), (2, 4, "bank3")])
+        value_banks = ([((0, 1, 2, 3), "bank4")], [((0, 1, 2, 3), "bank5")], [((0, 1, 2, 3), "bank6")], [((0, 1), "bank7"), ((2, 3), "bank0")])
 
         def second_product(c):
             z_words = sb(f"z_words{c}", [P, CHUNK], U32)
             z_scales = sb(f"z_scales{c}", [P, CHUNK], U8)
             nc.vector.quantize_mx(out=z_words[:].bitcast(FP8X4), scales=z_scales[:], in_=z_rounded[c][:].rearrange("p j t -> p (j t)"))
-            y_banks[c] = []
-            for lo, hi, bank_name in value_banks[c]:
-                bank = psum.tile([P, hi - lo, CHUNK], F32, name=bank_name)
-                for t in range(lo, hi):
-                    nc.tensor.matmul_mx(
-                        out=bank[:, t - lo, :],
-                        lhsT=values[:, t * P : (t + 1) * P].bitcast(FP8X4),
-                        lhsT_scale=value_scales[:, t * P : (t + 1) * P],
-                        rhs=z_words[:].bitcast(FP8X4),
-                        rhs_scale=z_scales[:],
-                        start=True,
-                        stop=True,
-                    )
-                y_banks[c].append((lo, hi, bank))
+            y_banks[c] = [(planes, product(name, values, value_scales, z_words[:], z_scales[:], planes)) for planes, name in value_banks[c]]
 
         def store_result(c):
             y_sb[c] = sb(f"y{c}", [P, PACK, CHUNK], F32)
-            for lo, hi, bank in y_banks[c]:
-                nc.scalar.copy(y_sb[c][:, lo:hi, :], bank[:])
-            nc.sync.dma_start(out_planes[:, :, c * CHUNK : (c + 1) * CHUNK], y_sb[c][:])
+            for planes, bank in y_banks[c]:
+                nc.scalar.copy(y_sb[c][:, planes[0] : planes[-1] + 1, :], bank[:])
+            nc.sync.dma_start(out_planes[:, :, columns(c)], y_sb[c][:])
 
-        def round_result(c):
+        def round_result(c, copy):
             y_rounded[c] = sb(f"y_rounded{c}", [P, CHUNK, PACK], BF16)
-            copy = nc.scalar.copy if c == 0 else nc.vector.tensor_copy
             copy(y_rounded[c][:].rearrange("p (c i) t -> p c t i", i=RUN), y_sb[c][:].rearrange("p t (c i) -> p c t i", i=RUN))
 
         def quantise_result(c):
             nc.vector.quantize_mx(
-                out=y_words[:, c * CHUNK : (c + 1) * CHUNK].bitcast(FP8X4),
-                scales=y_scales[:, c * CHUNK : (c + 1) * CHUNK],
+                out=y_words[:, columns(c)].bitcast(FP8X4),
+                scales=y_scales[:, columns(c)],
                 in_=y_rounded[c][:].rearrange("p j t -> p (j t)"),
             )
 
-        pick_queries(queries_first[:], 0, mid_lo)
-        bank_first0 = scores("bank0", (0,), queries_first[:], 0, mid_lo)
-        s_first1 = sb("s_first1", [P, 1, CHUNK], F32)
-        nc.scalar.copy(s_first1[:], scores("bank1", (1,), queries_first[:], 0, mid_lo)[:])
-        s_first23 = work.tile([P, 2, CHUNK], F32, name="s_first23", offset=2 * SLOT, align_bytes=64)
-        nc.scalar.copy(s_first23[:], scores("bank2", (2, 3), queries_first[:], 0, mid_lo)[:])
-        pick_queries(queries_rest[:], mid_lo, S)
-        queries_mid, queries_last = queries_rest[:, : 2 * CHUNK], queries_rest[:, 2 * CHUNK :]
-
-        def scores_rest(bank_name, t):
-            bank = psum.tile([P, 3 * CHUNK], F32, name=bank_name)
-            score_pass(bank[:, : 2 * CHUNK], t, queries_mid, mid_lo, last_lo)
-            score_pass(bank[:, 2 * CHUNK :], t, queries_last, last_lo, S)
-            return bank
-
-        bank_rest0 = scores_rest("bank3", 0)
-        bank_mid12 = scores("bank4", (1, 2), queries_mid, mid_lo, last_lo)
-        bank_mid3 = scores("bank5", (3,), queries_mid, mid_lo, last_lo)
-        bank_last = scores("bank6", (1, 2, 3), queries_last, last_lo, S)
-        temp_mid12 = work.tile([P, 2, 2 * CHUNK], F32, name="temp_mid12", offset=0, align_bytes=64)
-        temp_last = work.tile([P, 3, CHUNK], F32, name="temp_last", offset=6 * SLOT, align_bytes=64)
-        s_mid3 = work.tile([P, 2 * CHUNK], F32, name="s_mid3", offset=7 * SLOT // 4, align_bytes=64)
-
-        u_first = work.tile([P, PACK, CHUNK], F32, name="u_first", offset=6 * SLOT, align_bytes=64)
-        nc.vector.tensor_tensor(u_first[:, 0, :], bank_first0[:, 0, :], temp_first0[:], MULT)
-        look_up_times(u_first[:, 1, :], 1, 0, mid_lo, s_first1[:, 0, :])
-        for t in (2, 3):
-            look_up_times(u_first[:, t, :], t, 0, mid_lo, s_first23[:, t - 2, :])
-        tempered[0] = u_first[:]
-        for t in (1, 2):
-            look_up(temp_mid12[:, t - 1, :], t, mid_lo, last_lo)
-        squash(0)
-        nc.scalar.copy(s_mid3[:], bank_mid3[:, 0, :])
-        for t in (1, 2, 3):
-            look_up(temp_last[:, t - 1, :], t, last_lo, S)
-
-        u_rest = work.tile([P, PACK, 3 * CHUNK], F32, name="u_rest", offset=9 * SLOT // 4, align_bytes=64)
-        nc.vector.tensor_tensor(u_rest[:, 0, :], bank_rest0[:], temp_rest0[:], MULT)
-        nc.vector.tensor_tensor(u_rest[:, 1:3, : 2 * CHUNK], bank_mid12[:], temp_mid12[:], MULT)
-        look_up_times(u_rest[:, 3, : 2 * CHUNK], 3, mid_lo, last_lo, s_mid3[:])
-        gain(0, sb("z_rounded0", [P, CHUNK, PACK], BF16))
-        nc.vector.tensor_tensor(u_rest[:, 1:, 2 * CHUNK :], bank_last[:], temp_last[:], MULT)
+        pick_queries(queries_first[:], 0, CHUNK)
+        look_up(3, 0, CHUNK)
+        scores[0] = product("bank0", keys, key_scales, queries_first[:], query_scales[:, columns(0)], range(PACK))
+        pick_queries(queries_rest[:], CHUNK, S)
+        look_up(3, CHUNK, 3 * CHUNK)
         for c in range(1, 4):
-            tempered[c] = u_rest[:, :, (c - 1) * CHUNK : c * CHUNK]
+            scores[c] = product(f"bank{c}", keys, key_scales, queries_rest[:, columns(c - 1)], query_scales[:, columns(c)], range(PACK))
+        look_up(3, 3 * CHUNK, S)
         nc.vector.tensor_copy(
             values[:].bitcast(I32).rearrange("p (t c i) -> p c t i", t=PACK, i=LINE),
             w_words[:].rearrange("p (c i t) -> p c t i", t=PACK, i=LINE),
         )
-        for c in range(1, 4):
+        for c in range(3):
+            temper(c)
             squash(c)
-
+        gain(0)
+        temper(3)
+        squash(3)
         second_product(0)
-        gain(1, work.tile([P, CHUNK, PACK], BF16, name="z_rounded1", offset=7 * SLOT, align_bytes=64))
-        gain(2, sb("z_rounded2", [P, CHUNK, PACK], BF16))
+        gain(1)
+        gain(2)
         second_product(1)
         second_product(2)
-        gain(3, work.tile([P, CHUNK, PACK], BF16, name="z_rounded3", offset=7 * SLOT, align_bytes=64))
+        gain(3)
         store_result(0)
-        round_result(0)
+        round_result(0, nc.scalar.copy)
         quantise_result(0)
         nc.sync.dma_start(out_words[:, :CHUNK], y_words[:, :CHUNK])
         second_product(3)
         for c in range(1, 4):
             store_result(c)
-        round_result(1)
-        for c in range(2, 4):
-            round_result(c)
-            quantise_result(c - 1)
+        for c in range(1, 4):
+            round_result(c, nc.vector.tensor_copy)
+            if c > 1:
+                quantise_result(c - 1)
         quantise_result(3)
         nc.sync.dma_start(out_words[:, CHUNK:], y_words[:, CHUNK:])
         for q in range(4):

@@ -143,7 +143,9 @@ def tile_picked_temper_tanh_po_kernel(
 
         def temper(c):
             tempered[c] = sb(f"tempered{c}", [P, PACK, CHUNK], F32)
-            nc.vector.tensor_tensor(tempered[c][:], scores[c][:], temp_picked[:, :, columns(c)], MULT)
+            for planes, bank in scores[c]:
+                pair = slice(planes[0], planes[-1] + 1)
+                nc.vector.tensor_tensor(tempered[c][:, pair, :], bank[:], temp_picked[:, pair, columns(c)], MULT)
 
         def squash(c):
             squashed[c] = sb(f"squashed{c}", [P, PACK, CHUNK], F32)
@@ -185,41 +187,42 @@ def tile_picked_temper_tanh_po_kernel(
 
         pick_queries(queries_first[:], 0, CHUNK)
         look_up(3, 0, CHUNK)
-        scores[0] = product("bank0", keys, key_scales, queries_first[:], query_scales[:, columns(0)], range(PACK))
+        scores[0] = [
+            (planes, product(name, keys, key_scales, queries_first[:], query_scales[:, columns(0)], planes))
+            for planes, name in (((0, 1), "bank0"), ((2, 3), "bank7"))
+        ]
         pick_queries(queries_rest[:], CHUNK, S)
         look_up(3, CHUNK, 3 * CHUNK)
         for c in range(1, 4):
-            scores[c] = product(f"bank{c}", keys, key_scales, queries_rest[:, columns(c - 1)], query_scales[:, columns(c)], range(PACK))
+            scores[c] = [(range(PACK), product(f"bank{c}", keys, key_scales, queries_rest[:, columns(c - 1)], query_scales[:, columns(c)], range(PACK)))]
         look_up(3, 3 * CHUNK, S)
-        nc.vector.tensor_copy(
-            values[:].bitcast(I32).rearrange("p (t c i) -> p c t i", t=PACK, i=LINE),
-            w_words[:].rearrange("p (c i t) -> p c t i", t=PACK, i=LINE),
+        nc.scalar.copy(
+            values[:].rearrange("p (t c i) -> p c t i", t=PACK, i=LINE),
+            w_words[:].bitcast(U32).rearrange("p (c i t) -> p c t i", t=PACK, i=LINE),
         )
-        for c in range(3):
+        for c in range(4):
             temper(c)
             squash(c)
         gain(0)
-        temper(3)
-        squash(3)
-        second_product(0)
         gain(1)
+        second_product(0)
         gain(2)
         second_product(1)
         second_product(2)
         gain(3)
-        store_result(0)
-        round_result(0, nc.scalar.copy)
-        quantise_result(0)
-        nc.sync.dma_start(out_words[:, :CHUNK], y_words[:, :CHUNK])
         second_product(3)
-        for c in range(1, 4):
+        for c in range(4):
             store_result(c)
-        for c in range(1, 4):
-            round_result(c, nc.vector.tensor_copy)
-            if c > 1:
-                quantise_result(c - 1)
+        round_result(0, nc.vector.tensor_copy)
+        round_result(1, nc.vector.tensor_copy)
+        quantise_result(0)
+        quantise_result(1)
+        round_result(2, nc.vector.tensor_copy)
+        quantise_result(2)
+        nc.sync.dma_start(out_words[:, : 3 * CHUNK], y_words[:, : 3 * CHUNK])
+        round_result(3, nc.vector.tensor_copy)
         quantise_result(3)
-        nc.sync.dma_start(out_words[:, CHUNK:], y_words[:, CHUNK:])
+        nc.sync.dma_start(out_words[:, 3 * CHUNK :], y_words[:, 3 * CHUNK :])
         for q in range(4):
             queue = nc.scalar if q % 2 else nc.sync
             queue.dma_start(out_2[0, 4 * q : 4 * q + 4, :].bitcast(I32), y_scales[32 * q : 32 * q + 4, :].bitcast(I32))

@@ -113,7 +113,6 @@ def tile_picked_temper_tanh_po_kernel(
 
         queries_first = sb("queries_first", [P, CHUNK], U32)
         queries_rest = sb("queries_rest", [P, 3 * CHUNK], U32)
-        values = sb("values", [P, S], U32)
         y_scales = sb("y_scales", [P, S], U8)
         y_words = sb("y_words", [P, S], I32)
         out_planes = out_0.rearrange("(p t) j -> p t j", t=PACK)
@@ -142,7 +141,7 @@ def tile_picked_temper_tanh_po_kernel(
         scores, tempered, squashed, z_rounded, y_banks, y_sb, y_rounded = {}, {}, {}, {}, {}, {}, {}
 
         def temper(c):
-            tempered[c] = sb(f"tempered{c}", [P, PACK, CHUNK], F32)
+            tempered[c] = loads.tile([P, PACK, CHUNK], F32, name=f"tempered{c}", offset=(5 + c) * SLOT)
             for planes, bank in scores[c]:
                 pair = slice(planes[0], planes[-1] + 1)
                 nc.vector.tensor_tensor(tempered[c][:, pair, :], bank[:], temp_picked[:, pair, columns(c)], MULT)
@@ -191,23 +190,35 @@ def tile_picked_temper_tanh_po_kernel(
             (planes, product(name, keys, key_scales, queries_first[:], query_scales[:, columns(0)], planes))
             for planes, name in (((0, 1), "bank0"), ((2, 3), "bank7"))
         ]
-        pick_queries(queries_rest[:], CHUNK, S)
+        pick_queries(queries_rest[:, :CHUNK], CHUNK, HALF)
+        pick_queries(queries_rest[:, CHUNK:], HALF, S)
         look_up(3, CHUNK, 3 * CHUNK)
-        for c in range(1, 4):
-            scores[c] = [(range(PACK), product(f"bank{c}", keys, key_scales, queries_rest[:, columns(c - 1)], query_scales[:, columns(c)], range(PACK)))]
+
+        def score(c, bank_name):
+            bank = product(bank_name, keys, key_scales, queries_rest[:, columns(c - 1)], query_scales[:, columns(c)], range(PACK))
+            scores[c] = [(range(PACK), bank)]
+
+        score(1, "bank1")
+        score(2, "bank2")
         look_up(3, 3 * CHUNK, S)
+        temper(0)
+        squash(0)
+        for c in (1, 2):
+            temper(c)
+            squash(c)
+        values = loads.tile([P, S], U32, name="values", offset=7 * SLOT, align_bytes=64)
         nc.scalar.copy(
             values[:].rearrange("p (t c i) -> p c t i", t=PACK, i=LINE),
             w_words[:].bitcast(U32).rearrange("p (c i t) -> p c t i", t=PACK, i=LINE),
         )
-        for c in range(4):
-            temper(c)
-            squash(c)
+        score(3, "bank2")
         gain(0)
         gain(1)
         second_product(0)
-        gain(2)
+        temper(3)
+        squash(3)
         second_product(1)
+        gain(2)
         second_product(2)
         gain(3)
         second_product(3)

@@ -97,7 +97,7 @@ def tile_picked_temper_tanh_po_kernel(
         look_up(2, 0, HALF)
         look_up(2, HALF, S)
 
-        d_words_picked = sb("d_words_picked", [P, S], U32)
+        d_words_picked = loads.tile([P, S], U32, name="d_words_picked", offset=10 * SLOT - 64)
         keys = sb("keys", [P, S], U32)
         nc.vector.tensor_copy(d_words_picked[:], d_word_table[:].bitcast(U32).indirect(kidx_sb[:]))
         nc.vector.tensor_copy(value_scales[:].rearrange("p (t m) -> p t m", t=PACK), w_scale_rows[:].rearrange("p (m t) -> p t m", t=PACK))
@@ -105,9 +105,9 @@ def tile_picked_temper_tanh_po_kernel(
             keys[:].bitcast(I32).rearrange("p (t c i) -> p c t i", t=PACK, i=LINE),
             d_words_picked[:].bitcast(I32).rearrange("p (c i t) -> p c t i", t=PACK, i=LINE),
         )
-        w_words = loads.tile([P, S], I32, name="w_words", offset=SLOT + 64)
+        w_words = loads.tile([P, S], I32, name="w_words", offset=9 * SLOT)
         nc.sync.dma_start(w_words[:], words_of(w1_words))
-        gn_sb = loads.tile([P, PACK], F32, name="gn_sb", offset=SLOT)
+        gn_sb = loads.tile([P, PACK], F32, name="gn_sb", offset=10 * SLOT)
         nc.sync.dma_start(gn_sb[:], gn.rearrange("(p t) o -> p (t o)", t=PACK))
         move_scale_rows(value_scales, nc.sync)
 

from contextlib import ExitStack

import concourse.mybir as mybir

F32 = mybir.dt.float32
BF16 = mybir.dt.bfloat16
I32 = mybir.dt.int32
U32 = mybir.dt.uint32
U16 = mybir.dt.uint16
U8 = mybir.dt.uint8
FP8X4 = mybir.dt.float8_e4m3fn_x4
ACT = mybir.ActivationFunctionType
MULT = mybir.AluOpType.mult

P = 128
PACK = 4
TABLE = 2048
S = 512
CHUNK = 128
HALF = S // 2
LINE = 4
RUN = 2
SLOT = 2048
FLOPS = 2 * 2 * 512 * 512 * 512


def words_of(dram):
    return dram[0].rearrange("p n t -> p (n t)").bitcast(I32)


def entries(list_sb, lo, hi):
    return list_sb[:, lo // 16 : hi // 16]


def tile_picked_temper_tanh_po_kernel(
    tc, x_words, x_scales, d_words, d_scales, temp, gn, w1_words, w1_scales, offs, kidx, task, out_0, out_1, out_2
):
    nc = tc.nc
    with ExitStack() as ctx:
        keep = ctx.enter_context(tc.tile_pool(name="keep", bufs=1))
        loads = ctx.enter_context(tc.tile_pool(name="loads", bufs=1))
        psum = ctx.enter_context(tc.psum_pool(name="psum", bufs=1))

        def sb(name, shape, dtype):
            return keep.tile(shape, dtype, name=name, align_bytes=64)

        def move_scale_rows(tile, queue):
            for r in range(1, PACK):
                queue.dma_start(tile[r:P:32, :].bitcast(I32), tile[8 * r : P : 32, :].bitcast(I32))

        kidx_sb = sb("kidx_sb", [P, S // 16], U16)
        offs_sb = sb("offs_sb", [P, S // 16], U16)
        task_sb = sb("task_sb", [P, S // 16], U16)
        d_scale_table = sb("d_scale_table", [P, TABLE], U8)
        x_scale_table = sb("x_scale_table", [P, TABLE], U8)
        w_scale_rows = sb("w_scale_rows", [P, S], U8)
        d_word_table = loads.tile([P, TABLE], I32, name="d_word_table", offset=0)
        x_word_table = sb("x_word_table", [P, TABLE], I32)
        for rows in (d_scale_table, x_scale_table, w_scale_rows):
            nc.vector.memset(rows[:].bitcast(I32), 0)
        temp_planes = temp.rearrange("(p t) u -> p t u", t=PACK)
        temp_sb = [sb(f"temp{t}", [P, S], F32) for t in range(PACK)]
        nc.sync.dma_start(temp_sb[0][:], temp_planes[:, 0, :])
        nc.sync.dma_start(kidx_sb[:], kidx)
        nc.sync.dma_start(offs_sb[:], offs)
        nc.sync.dma_start(task_sb[:], task)
        nc.sync.dma_start(d_scale_table[0:P:8, :].bitcast(I32), d_scales[0].bitcast(I32))
        nc.sync.dma_start(temp_sb[1][:], temp_planes[:, 1, :])
        nc.sync.dma_start(x_scale_table[0:P:8, :].bitcast(I32), x_scales[0].bitcast(I32))
        nc.sync.dma_start(d_word_table[:], words_of(d_words))
        nc.sync.dma_start(w_scale_rows[0:P:8, :].bitcast(I32), w1_scales[0].bitcast(I32))
        nc.sync.dma_start(temp_sb[2][:], temp_planes[:, 2, :])
        nc.sync.dma_start(x_word_table[:], words_of(x_words))
        nc.sync.dma_start(temp_sb[3][:], temp_planes[:, 3, :])

        temp_picked = sb("temp_picked", [P, PACK, S], F32)

        def look_up(t, lo, hi):
            nc.scalar.activation(temp_picked[:, t, lo:hi], temp_sb[t][:].indirect(entries(task_sb, lo, hi)), ACT.Copy)

        for t in range(2):
            look_up(t, 0, HALF)
            look_up(t, HALF, S)

        scales = sb("scales", [P, 2 * S], U8)
        key_scales, query_scales = scales[:, :S], scales[:, S:]
        value_scales = sb("value_scales", [P, S], U8)
        d_scales_picked = sb("d_scales_picked", [P, S], U8)
        x_scales_picked = sb("x_scales_picked", [P, S], U8)
        nc.vector.tensor_copy(d_scales_picked[:], d_scale_table[:].indirect(kidx_sb[:]))
        nc.vector.tensor_copy(x_scales_picked[:], x_scale_table[:].indirect(offs_sb[:]))
        nc.vector.tensor_copy(
            key_scales.rearrange("p (t m) -> p t m", t=PACK), d_scales_picked[:].rearrange("p (m t) -> p t m", t=PACK)
        )
        nc.vector.tensor_copy(query_scales.bitcast(I32), x_scales_picked[:].bitcast(I32))
        move_scale_rows(scales, nc.scalar)
        look_up(2, 0, HALF)
        look_up(2, HALF, S)

        d_words_picked = loads.tile([P, S], U32, name="d_words_picked", offset=10 * SLOT - 64)
        keys = sb("keys", [P, S], U32)
        nc.vector.tensor_copy(d_words_picked[:], d_word_table[:].bitcast(U32).indirect(kidx_sb[:]))
        nc.vector.tensor_copy(value_scales[:].rearrange("p (t m) -> p t m", t=PACK), w_scale_rows[:].rearrange("p (m t) -> p t m", t=PACK))
        nc.vector.tensor_copy(
            keys[:].bitcast(I32).rearrange("p (t c i) -> p c t i", t=PACK, i=LINE),
            d_words_picked[:].bitcast(I32).rearrange("p (c i t) -> p c t i", t=PACK, i=LINE),
        )
        w_words = loads.tile([P, S], I32, name="w_words", offset=9 * SLOT)
        nc.sync.dma_start(w_words[:], words_of(w1_words))
        gn_sb = loads.tile([P, PACK], F32, name="gn_sb", offset=10 * SLOT)
        nc.sync.dma_start(gn_sb[:], gn.rearrange("(p t) o -> p (t o)", t=PACK))
        move_scale_rows(value_scales, nc.sync)

        queries_first = sb("queries_first", [P, CHUNK], U32)
        queries_rest = sb("queries_rest", [P, 3 * CHUNK], U32)
        y_scales = sb("y_scales", [P, S], U8)
        y_words = sb("y_words", [P, S], I32)
        out_planes = out_0.rearrange("(p t) j -> p t j", t=PACK)
        out_words = words_of(out_1)

        def pick_queries(out, lo, hi):
            nc.vector.tensor_copy(out, x_word_table[:].bitcast(U32).indirect(entries(offs_sb, lo, hi)))

        def product(bank_name, stationary, stationary_scales, moving, moving_scales, planes):
            bank = psum.tile([P, len(planes), CHUNK], F32, name=bank_name)
            for e, t in enumerate(planes):
                nc.tensor.matmul_mx(
                    out=bank[:, e, :],
                    lhsT=stationary[:, t * P : (t + 1) * P].bitcast(FP8X4),
                    lhsT_scale=stationary_scales[:, t * P : (t + 1) * P],
                    rhs=moving.bitcast(FP8X4),
                    rhs_scale=moving_scales,
                    start=True,
                    stop=True,
                )
            return bank

        def columns(c):
            return slice(c * CHUNK, (c + 1) * CHUNK)

        scores, tempered, squashed, z_rounded, y_banks, y_sb, y_rounded = {}, {}, {}, {}, {}, {}, {}

        def temper(c):
            tempered[c] = loads.tile([P, PACK, CHUNK], F32, name=f"tempered{c}", offset=(5 + c) * SLOT)
            for planes, bank in scores[c]:
                pair = slice(planes[0], planes[-1] + 1)
                nc.vector.tensor_tensor(tempered[c][:, pair, :], bank[:], temp_picked[:, pair, columns(c)], MULT)

        def squash(c):
            squashed[c] = sb(f"squashed{c}", [P, PACK, CHUNK], F32)
            nc.scalar.activation(squashed[c][:], tempered[c][:], ACT.Tanh, scale=0.0625)

        def gain(c):
            z_rounded[c] = sb(f"z_rounded{c}", [P, CHUNK, PACK], BF16)
            nc.vector.tensor_tensor(
                z_rounded[c][:].rearrange("p (c i) t -> p c t i", i=RUN),
                squashed[c][:].rearrange("p t (c i) -> p c t i", i=RUN),
                gn_sb[:].unsqueeze(1).unsqueeze(3).to_broadcast([P, CHUNK // RUN, PACK, RUN]),
                MULT,
            )

        value_banks = ([((0, 1, 2, 3), "bank4")], [((0, 1, 2, 3), "bank5")], [((0, 1, 2, 3), "bank6")], [((0, 1), "bank7"), ((2, 3), "bank0")])

        def second_product(c):
            z_words = sb(f"z_words{c}", [P, CHUNK], U32)
            z_scales = sb(f"z_scales{c}", [P, CHUNK], U8)
            nc.vector.quantize_mx(out=z_words[:].bitcast(FP8X4), scales=z_scales[:], in_=z_rounded[c][:].rearrange("p j t -> p (j t)"))
            y_banks[c] = [(planes, product(name, values, value_scales, z_words[:], z_scales[:], planes)) for planes, name in value_banks[c]]

        def store_result(c):
            y_sb[c] = sb(f"y{c}", [P, PACK, CHUNK], F32)
            for planes, bank in y_banks[c]:
                nc.scalar.copy(y_sb[c][:, planes[0] : planes[-1] + 1, :], bank[:])
            nc.sync.dma_start(out_planes[:, :, columns(c)], y_sb[c][:])

        def round_result(c, copy):
            y_rounded[c] = sb(f"y_rounded{c}", [P, CHUNK, PACK], BF16)
            copy(y_rounded[c][:].rearrange("p (c i) t -> p c t i", i=RUN), y_sb[c][:].rearrange("p t (c i) -> p c t i", i=RUN))

        def quantise_result(c):
            nc.vector.quantize_mx(
                out=y_words[:, columns(c)].bitcast(FP8X4),
                scales=y_scales[:, columns(c)],
                in_=y_rounded[c][:].rearrange("p j t -> p (j t)"),
            )

        pick_queries(queries_first[:], 0, CHUNK)
        look_up(3, 0, CHUNK)
        scores[0] = [
            (planes, product(name, keys, key_scales, queries_first[:], query_scales[:, columns(0)], planes))
            for planes, name in (((0, 1), "bank0"), ((2, 3), "bank7"))
        ]
        pick_queries(queries_rest[:, :CHUNK], CHUNK, HALF)
        pick_queries(queries_rest[:, CHUNK:], HALF, S)
        look_up(3, CHUNK, 3 * CHUNK)

        def score(c, bank_name):
            bank = product(bank_name, keys, key_scales, queries_rest[:, columns(c - 1)], query_scales[:, columns(c)], range(PACK))
            scores[c] = [(range(PACK), bank)]

        score(1, "bank1")
        score(2, "bank2")
        look_up(3, 3 * CHUNK, S)
        temper(0)
        squash(0)
        for c in (1, 2):
            temper(c)
            squash(c)
        values = loads.tile([P, S], U32, name="values", offset=7 * SLOT, align_bytes=64)
        nc.scalar.copy(
            values[:].rearrange("p (t c i) -> p c t i", t=PACK, i=LINE),
            w_words[:].bitcast(U32).rearrange("p (c i t) -> p c t i", t=PACK, i=LINE),
        )
        score(3, "bank2")
        gain(0)
        gain(1)
        second_product(0)
        temper(3)
        squash(3)
        second_product(1)
        gain(2)
        second_product(2)
        gain(3)
        second_product(3)
        for c in range(4):
            store_result(c)
        round_result(0, nc.vector.tensor_copy)
        round_result(1, nc.vector.tensor_copy)
        quantise_result(0)
        quantise_result(1)
        round_result(2, nc.vector.tensor_copy)
        quantise_result(2)
        nc.sync.dma_start(out_words[:, : 3 * CHUNK], y_words[:, : 3 * CHUNK])
        round_result(3, nc.vector.tensor_copy)
        quantise_result(3)
        nc.sync.dma_start(out_words[:, 3 * CHUNK :], y_words[:, 3 * CHUNK :])
        for q in range(4):
            queue = nc.scalar if q % 2 else nc.sync
            queue.dma_start(out_2[0, 4 * q : 4 * q + 4, :].bitcast(I32), y_scales[32 * q : 32 * q + 4, :].bitcast(I32))
